import numpy as np
import ml_dtypes


def mxq(x, axis, fmt="e4m3"):
    dtype, down = {"e4m3": (ml_dtypes.float8_e4m3fn, 7), "e5m2": (ml_dtypes.float8_e5m2, 14)}[fmt]
    v = np.moveaxis(np.asarray(x, np.float32).astype(ml_dtypes.bfloat16).astype(np.float64), axis, -1)
    blocks = v.reshape(v.shape[:-1] + (-1, 32))
    amax = np.abs(blocks).max(-1, keepdims=True)
    byte = np.maximum(np.where(amax > 0, np.frexp(amax)[1] - 1 + 127, 0) - down, 1)
    scale = np.exp2(byte - 127.0)
    codes = (blocks / scale).astype(np.float32).astype(dtype).astype(np.float64)
    return np.moveaxis((codes * scale).reshape(v.shape), -1, axis)


WIDE = False


def mx_kscale(k):
    if not WIDE:
        return np.ones(k)
    levels = np.array([10, -10, 5, -5, 0])
    if k % 512:
        return np.exp2(np.random.permutation(np.resize(levels, k // 32))).repeat(32)
    a = np.empty((k // 512, 16))
    for p in range(k // 512):
        a[p, :8] = np.random.permutation(np.resize(levels, 8))
        for g in range(8):
            far = levels[np.abs(levels - a[p, g]) >= 10]
            a[p, g + 8] = far[np.random.randint(len(far))]
    return np.exp2(a.ravel()).repeat(32)


def f64(x):
    return np.asarray(x).astype(np.float64)


def striped(idx):
    return np.tile(idx.reshape(-1, 16).T, (8, 1)).astype(np.uint16)


def unstriped(offs):
    return offs[:16].T.reshape(-1).astype(np.int64)


E2M1 = np.array([0.0, 0.5, 1.0, 1.5, 2.0, 3.0, 4.0, 6.0, -0.0, -0.5, -1.0, -1.5, -2.0, -3.0, -4.0, -6.0])


def pack_weight(w, fmt):
    k, n = w.shape
    w = f64(np.asarray(w, np.float32).astype(ml_dtypes.bfloat16)).reshape(k // 32, 32, n)
    amax = np.abs(w).max(1)
    if fmt == "e4m3":
        byte = np.frexp(amax)[1] - 1 + 127 - 7
    else:
        mant, ex = np.frexp(amax / 6.0)
        byte = np.where(mant > 0.5, ex, ex - 1) + 127
    byte = np.clip(np.where(amax > 0, byte, 1), 1, 254)
    scaled = (w * np.exp2(127.0 - byte)[:, None, :]).reshape(k, n).astype(np.float32)
    by_word = np.ascontiguousarray(scaled.reshape(k // 512, 128, 4, n).transpose(0, 1, 3, 2))
    if fmt == "e4m3":
        words = by_word.astype(ml_dtypes.float8_e4m3fn).view(np.uint8)
    else:
        c = by_word.astype(ml_dtypes.float4_e2m1fn).view(np.uint8) & 0xF
        words = (c[..., 0::2] | (c[..., 1::2] << 4)).reshape(k // 512, 128, 2 * n)
    return np.ascontiguousarray(words), np.ascontiguousarray(byte.astype(np.uint8).reshape(k // 512, 16, n))


def unpack_weight(words, scales, fmt):
    g, _, n = scales.shape
    words = np.ascontiguousarray(words).reshape(g, 128, n, -1)
    if fmt == "e4m3":
        vals = words.view(ml_dtypes.float8_e4m3fn).astype(np.float64)
    else:
        nib = np.empty((g, 128, n, 4), np.uint8)
        nib[..., 0::2] = words & 0xF
        nib[..., 1::2] = words >> 4
        vals = E2M1[nib]
    vals = vals * np.repeat(np.exp2(scales.astype(np.float64) - 127.0), 8, axis=1)[..., None]
    return vals.transpose(0, 1, 3, 2).reshape(g * 512, n)


K, T, E, B, H, N = 512, 512, 8, 4, 512, 256


def setup_inputs():
    n = np.random.standard_normal
    s = mx_kscale(K)
    u = mx_kscale(H)
    slot_token = np.random.permutation(T)[:128 * B]
    block = np.sort(np.random.randint(E, size=B))
    x = pack_weight(n((K, T)) * s[:, None], "e4m3")
    w1 = pack_weight(n((K, E * H)) / np.sqrt(K) / s[:, None] * np.tile(u, E), "e4m3")
    w2 = pack_weight(n((H, E * N)) / np.sqrt(H) / u[:, None], "e4m3")
    return {
        "x_words": x[0],
        "x_scales": x[1],
        "w1_words": w1[0],
        "w1_scales": w1[1],
        "w2_words": w2[0],
        "w2_scales": w2[1],
        "gate": (np.tile(np.random.uniform(0.2, 1.0, 128 * B), (128, 1))).astype(np.float32),
        "offs": striped(slot_token),
        "offs2": striped((block[:, None] * H + np.arange(H)).reshape(-1)),
        "offs3": striped((block[:, None] * N + np.arange(N)).reshape(-1)),
    }


def reference(x_words, x_scales, w1_words, w1_scales, w2_words, w2_scales, gate, offs, offs2, offs3):
    idx, idx2, idx3 = unstriped(offs), unstriped(offs2), unstriped(offs3)
    xq = unpack_weight(x_words, x_scales, "e4m3")[:, idx]
    w1 = unpack_weight(w1_words, w1_scales, "e4m3")[:, idx2]
    w2 = unpack_weight(w2_words, w2_scales, "e4m3")[:, idx3]
    h = np.concatenate([w1[:, m * H:(m + 1) * H].T @ xq[:, 128 * m:128 * m + 128] for m in range(B)], axis=1)
    hq = mxq(h, 0, "e4m3")
    y = np.concatenate([w2[:, m * N:(m + 1) * N].T @ hq[:, 128 * m:128 * m + 128] for m in range(B)], axis=1)
    out = np.zeros((N, T))
    out[:, idx] = f64(gate[:1]) * y
    return out

@@ -1,0 +1,147 @@
+from contextlib import ExitStack
+
+import concourse.mybir as mybir
+from concourse.masks import make_identity
+
+K, T, E, B, H, N = 512, 512, 8, 4, 512, 256
+FLOPS = 2 * T * K * H + 2 * T * H * N
+
+F32 = mybir.dt.float32
+BF16 = mybir.dt.bfloat16
+I32 = mybir.dt.int32
+U32 = mybir.dt.uint32
+U16 = mybir.dt.uint16
+U8 = mybir.dt.uint8
+FP8X4 = mybir.dt.float8_e4m3fn_x4
+
+P = 128
+SLOTS = 128
+PER_COL = 16
+X_WINDOW = 768
+PAIR = 2 * SLOTS
+
+
+def load_list(nc, pool, source, name):
+    offsets = pool.tile(list(source.shape), U16, name=name)
+    nc.sync.dma_start(offsets[:], source)
+    return offsets
+
+
+def entries(offsets, first, count):
+    return offsets[:, first // PER_COL : (first + count) // PER_COL]
+
+
+def words_in_hbm(words):
+    return words[0].rearrange("p c d -> p (c d)").bitcast(I32)
+
+
+def load_scale_rows(nc, plane, scales):
+    width = scales.shape[2]
+    for r in range(4):
+        nc.scalar.dma_start(plane[r:P:32, 0:width].bitcast(I32), scales[0, r:16:4, :].bitcast(I32))
+
+
+def tile_moe_dyn_none_kernel(
+    tc, x_words, x_scales, w1_words, w1_scales, w2_words, w2_scales, gate, offs, offs2, offs3, out
+):
+    nc = tc.nc
+    with ExitStack() as ctx:
+        keep = ctx.enter_context(tc.tile_pool(name="keep", bufs=1))
+        ring = ctx.enter_context(tc.tile_pool(name="ring", bufs=2))
+        psum2 = ctx.enter_context(tc.psum_pool(name="psum2", bufs=2))
+        psum1 = ctx.enter_context(tc.psum_pool(name="psum1", bufs=1))
+
+        w1_plane = keep.tile([P, E * H], U8, align_bytes=64)
+        x_table = keep.tile([P, X_WINDOW], I32, align_bytes=64, tag="table")
+        x_plane = keep.tile([P, X_WINDOW], U8, align_bytes=64, tag="late")
+        w2_plane = keep.tile([P, E * N], U8, align_bytes=64)
+        w1_table = keep.tile([P, E * H], I32, align_bytes=64)
+        nc.vector.memset(w1_plane[:].bitcast(I32), 0)
+        nc.vector.memset(x_table[:, T:X_WINDOW], 0)
+        nc.vector.memset(x_plane[:].bitcast(I32), 0)
+        nc.vector.memset(w2_plane[:].bitcast(I32), 0)
+
+        tok = load_list(nc, keep, offs, "tok")
+        nc.sync.dma_start(x_table[:, 0:T], words_in_hbm(x_words))
+        col1 = load_list(nc, keep, offs2, "col1")
+        col2 = load_list(nc, keep, offs3, "col2")
+        nc.sync.dma_start(w1_table[:], words_in_hbm(w1_words))
+        load_scale_rows(nc, w1_plane, w1_scales)
+        load_scale_rows(nc, x_plane, x_scales)
+        load_scale_rows(nc, w2_plane, w2_scales)
+
+        identity = keep.tile([P, P], F32)
+        make_identity(nc, identity[:])
+
+        x_codes = keep.tile([P, T], U32, align_bytes=64)
+        nc.vector.tensor_copy(x_codes[:], x_table[:].bitcast(U32).indirect(tok[:]))
+        w2_table = keep.tile([P, E * N], I32, align_bytes=64, tag="table")
+        nc.sync.dma_start(w2_table[:], words_in_hbm(w2_words))
+
+        w1_scale = keep.tile([P, B * H], U8, align_bytes=64)
+        nc.vector.tensor_copy(w1_scale[:], w1_plane[:].indirect(col1[:]))
+        x_scale = keep.tile([P, T], U8, align_bytes=64)
+        nc.vector.tensor_copy(x_scale[:], x_plane[:].indirect(tok[:]))
+        gates = keep.tile([P, T], F32, align_bytes=64, tag="late")
+        nc.sync.dma_start(gates[:], gate)
+
+        grouped = [keep.tile([P, PAIR * 4], BF16, align_bytes=64, name=f"grouped{g}", tag=f"grouped{g}") for g in range(2)]
+        for m in range(B):
+            slots = slice(m * SLOTS, (m + 1) * SLOTS)
+            w1_codes = keep.tile([P, H], U32, align_bytes=64, name=f"w1_codes{m}")
+            nc.vector.tensor_copy(w1_codes[:], w1_table[:].bitcast(U32).indirect(entries(col1, m * H, H)))
+            h_t = psum2.tile([P, H], F32)
+            nc.tensor.matmul_mx(
+                out=h_t[:],
+                lhsT=x_codes[:, slots].bitcast(FP8X4),
+                lhsT_scale=x_scale[:, slots],
+                rhs=w1_codes[:].bitcast(FP8X4),
+                rhs_scale=w1_scale[:, m * H : (m + 1) * H],
+                start=True,
+                stop=True,
+            )
+            rounded = ring.tile([P, H], BF16, align_bytes=64)
+            nc.scalar.copy(
+                rounded[:].rearrange("s (u p e) -> s u p e", u=2, e=2),
+                h_t[:].rearrange("s (p u e) -> s u p e", u=2, e=2),
+            )
+            turned = psum2.tile([P, 2, SLOTS], F32)
+            for u in range(2):
+                nc.tensor.transpose(turned[:, u, :], rounded[:].bitcast(F32)[:, u * P : (u + 1) * P], identity[:])
+            half = grouped[m // 2][:].bitcast(F32)[:, (m % 2) * 2 * SLOTS : (m % 2 + 1) * 2 * SLOTS]
+            nc.scalar.copy(half.rearrange("p (s u) -> p s u", u=2), turned[:].rearrange("p u s -> p s u"))
+
+        w2_scale = keep.tile([P, B * N], U8, align_bytes=64)
+        nc.vector.tensor_copy(w2_scale[:], w2_plane[:].indirect(col2[:]))
+
+        results = [keep.tile([P, T], F32, name=f"result{c}") for c in range(N // P)]
+        for g in range(2):
+            w2_codes = keep.tile([P, 2 * N], U32, align_bytes=64, name=f"w2_codes{g}", tag=("w2_first" if g == 0 else "grouped0"))
+            nc.vector.tensor_copy(w2_codes[:], w2_table[:].bitcast(U32).indirect(entries(col2, g * 2 * N, 2 * N)))
+            h_codes = keep.tile([P, PAIR], U32, align_bytes=64, name=f"h_codes{g}")
+            h_scale = keep.tile([P, PAIR], U8, align_bytes=64, name=f"h_scale{g}")
+            nc.vector.quantize_mx(out=h_codes[:].bitcast(FP8X4), scales=h_scale[:], in_=grouped[g][:])
+            for c in range(N // P):
+                y = psum1.tile([P, PAIR], F32, name=f"y{g}{c}")
+                for j in range(2):
+                    slots = slice(j * SLOTS, (j + 1) * SLOTS)
+                    cols = j * N + c * P
+                    nc.tensor.matmul_mx(
+                        out=y[:, slots],
+                        lhsT=w2_codes[:, cols : cols + P].bitcast(FP8X4),
+                        lhsT_scale=w2_scale[:, g * 2 * N + cols : g * 2 * N + cols + P],
+                        rhs=h_codes[:, slots].bitcast(FP8X4),
+                        rhs_scale=h_scale[:, slots],
+                        start=True,
+                        stop=True,
+                    )
+                y_sb = keep.tile([P, PAIR], F32, name=f"y_sb{g}{c}")
+                nc.scalar.copy(y_sb[:], y[:])
+                nc.vector.tensor_tensor(
+                    results[c][:].indirect(entries(tok, g * PAIR, PAIR)),
+                    y_sb[:],
+                    gates[:, g * PAIR : (g + 1) * PAIR],
+                    mybir.AluOpType.mult,
+                )
+        for c in range(N // P):
+            nc.sync.dma_start(out[c * P : (c + 1) * P, :], results[c][:])

@@ -51,11 +51,10 @@ def tile_moe_dyn_none_kernel(
         psum2 = ctx.enter_context(tc.psum_pool(name="psum2", bufs=2))
         psum1 = ctx.enter_context(tc.psum_pool(name="psum1", bufs=1))
 
-        w1_plane = keep.tile([P, E * H], U8, align_bytes=64)
-        x_table = keep.tile([P, X_WINDOW], I32, align_bytes=64, tag="table")
-        x_plane = keep.tile([P, X_WINDOW], U8, align_bytes=64, tag="late")
+        w1_plane = keep.tile([P, E * H], U8, align_bytes=64, tag="w1_plane_then_gates")
+        x_table = keep.tile([P, X_WINDOW], I32, align_bytes=64, tag="x_then_w1")
+        x_plane = keep.tile([P, X_WINDOW], U8, align_bytes=64, tag="x_plane_then_w2")
         w2_plane = keep.tile([P, E * N], U8, align_bytes=64)
-        w1_table = keep.tile([P, E * H], I32, align_bytes=64)
         nc.vector.memset(w1_plane[:].bitcast(I32), 0)
         nc.vector.memset(x_table[:, T:X_WINDOW], 0)
         nc.vector.memset(x_plane[:].bitcast(I32), 0)
@@ -65,7 +64,6 @@ def tile_moe_dyn_none_kernel(
         nc.sync.dma_start(x_table[:, 0:T], words_in_hbm(x_words))
         col1 = load_list(nc, keep, offs2, "col1")
         col2 = load_list(nc, keep, offs3, "col2")
-        nc.sync.dma_start(w1_table[:], words_in_hbm(w1_words))
         load_scale_rows(nc, w1_plane, w1_scales)
         load_scale_rows(nc, x_plane, x_scales)
         load_scale_rows(nc, w2_plane, w2_scales)
@@ -75,14 +73,16 @@ def tile_moe_dyn_none_kernel(
 
         x_codes = keep.tile([P, T], U32, align_bytes=64)
         nc.vector.tensor_copy(x_codes[:], x_table[:].bitcast(U32).indirect(tok[:]))
-        w2_table = keep.tile([P, E * N], I32, align_bytes=64, tag="table")
-        nc.sync.dma_start(w2_table[:], words_in_hbm(w2_words))
+        w1_table = keep.tile([P, E * H], I32, align_bytes=64, tag="x_then_w1")
+        nc.sync.dma_start(w1_table[:], words_in_hbm(w1_words))
 
         w1_scale = keep.tile([P, B * H], U8, align_bytes=64)
         nc.vector.tensor_copy(w1_scale[:], w1_plane[:].indirect(col1[:]))
         x_scale = keep.tile([P, T], U8, align_bytes=64)
         nc.vector.tensor_copy(x_scale[:], x_plane[:].indirect(tok[:]))
-        gates = keep.tile([P, T], F32, align_bytes=64, tag="late")
+        w2_table = keep.tile([P, E * N], I32, align_bytes=64, tag="x_plane_then_w2")
+        nc.sync.dma_start(w2_table[:], words_in_hbm(w2_words))
+        gates = keep.tile([P, T], F32, align_bytes=64, tag="w1_plane_then_gates")
         nc.sync.dma_start(gates[:], gate)
 
         grouped = [keep.tile([P, PAIR * 4], BF16, align_bytes=64, name=f"grouped{g}", tag=f"grouped{g}") for g in range(2)]

@@ -35,10 +35,10 @@ def words_in_hbm(words):
     return words[0].rearrange("p c d -> p (c d)").bitcast(I32)
 
 
-def load_scale_rows(nc, plane, scales):
+def load_scale_rows(queue, plane, scales):
     width = scales.shape[2]
     for r in range(4):
-        nc.scalar.dma_start(plane[r:P:32, 0:width].bitcast(I32), scales[0, r:16:4, :].bitcast(I32))
+        queue.dma_start(plane[r:P:32, 0:width].bitcast(I32), scales[0, r:16:4, :].bitcast(I32))
 
 
 def tile_moe_dyn_none_kernel(
@@ -47,7 +47,6 @@ def tile_moe_dyn_none_kernel(
     nc = tc.nc
     with ExitStack() as ctx:
         keep = ctx.enter_context(tc.tile_pool(name="keep", bufs=1))
-        ring = ctx.enter_context(tc.tile_pool(name="ring", bufs=2))
         psum2 = ctx.enter_context(tc.psum_pool(name="psum2", bufs=2))
         psum1 = ctx.enter_context(tc.psum_pool(name="psum1", bufs=1))
 
@@ -64,9 +63,9 @@ def tile_moe_dyn_none_kernel(
         nc.sync.dma_start(x_table[:, 0:T], words_in_hbm(x_words))
         col1 = load_list(nc, keep, offs2, "col1")
         col2 = load_list(nc, keep, offs3, "col2")
-        load_scale_rows(nc, w1_plane, w1_scales)
-        load_scale_rows(nc, x_plane, x_scales)
-        load_scale_rows(nc, w2_plane, w2_scales)
+        load_scale_rows(nc.sync, w1_plane, w1_scales)
+        load_scale_rows(nc.sync, x_plane, x_scales)
+        load_scale_rows(nc.sync, w2_plane, w2_scales)
 
         identity = keep.tile([P, P], F32)
         make_identity(nc, identity[:])
@@ -85,10 +84,13 @@ def tile_moe_dyn_none_kernel(
         gates = keep.tile([P, T], F32, align_bytes=64, tag="w1_plane_then_gates")
         nc.sync.dma_start(gates[:], gate)
 
+        w2_scale_first = keep.tile([P, 2 * N], U8, align_bytes=64)
+        nc.vector.tensor_copy(w2_scale_first[:], w2_plane[:].indirect(entries(col2, 0, 2 * N)))
+
         grouped = [keep.tile([P, PAIR * 4], BF16, align_bytes=64, name=f"grouped{g}", tag=f"grouped{g}") for g in range(2)]
         for m in range(B):
             slots = slice(m * SLOTS, (m + 1) * SLOTS)
-            w1_codes = keep.tile([P, H], U32, align_bytes=64, name=f"w1_codes{m}")
+            w1_codes = keep.tile([P, H], U32, align_bytes=64, name=f"w1_codes{m}", tag=f"w1_codes{m}")
             nc.vector.tensor_copy(w1_codes[:], w1_table[:].bitcast(U32).indirect(entries(col1, m * H, H)))
             h_t = psum2.tile([P, H], F32)
             nc.tensor.matmul_mx(
@@ -100,7 +102,7 @@ def tile_moe_dyn_none_kernel(
                 start=True,
                 stop=True,
             )
-            rounded = ring.tile([P, H], BF16, align_bytes=64)
+            rounded = keep.tile([P, H], BF16, align_bytes=64, name=f"rounded{m}", tag=f"rounded{m}")
             nc.scalar.copy(
                 rounded[:].rearrange("s (u p e) -> s u p e", u=2, e=2),
                 h_t[:].rearrange("s (p u e) -> s u p e", u=2, e=2),
@@ -111,12 +113,12 @@ def tile_moe_dyn_none_kernel(
             half = grouped[m // 2][:].bitcast(F32)[:, (m % 2) * 2 * SLOTS : (m % 2 + 1) * 2 * SLOTS]
             nc.scalar.copy(half.rearrange("p (s u) -> p s u", u=2), turned[:].rearrange("p u s -> p s u"))
 
-        w2_scale = keep.tile([P, B * N], U8, align_bytes=64)
-        nc.vector.tensor_copy(w2_scale[:], w2_plane[:].indirect(col2[:]))
-
-        results = [keep.tile([P, T], F32, name=f"result{c}") for c in range(N // P)]
+        w2_scale_second = keep.tile([P, 2 * N], U8, align_bytes=64, tag="w1_codes1")
+        nc.vector.tensor_copy(w2_scale_second[:], w2_plane[:].indirect(entries(col2, 2 * N, 2 * N)))
+        w2_scale = [w2_scale_first, w2_scale_second]
+        staged = {}
         for g in range(2):
-            w2_codes = keep.tile([P, 2 * N], U32, align_bytes=64, name=f"w2_codes{g}", tag=("w2_first" if g == 0 else "grouped0"))
+            w2_codes = keep.tile([P, 2 * N], U32, align_bytes=64, name=f"w2_codes{g}", tag=("w1_codes0" if g == 0 else "rounded2"))
             nc.vector.tensor_copy(w2_codes[:], w2_table[:].bitcast(U32).indirect(entries(col2, g * 2 * N, 2 * N)))
             h_codes = keep.tile([P, PAIR], U32, align_bytes=64, name=f"h_codes{g}")
             h_scale = keep.tile([P, PAIR], U8, align_bytes=64, name=f"h_scale{g}")
@@ -129,7 +131,7 @@ def tile_moe_dyn_none_kernel(
                     nc.tensor.matmul_mx(
                         out=y[:, slots],
                         lhsT=w2_codes[:, cols : cols + P].bitcast(FP8X4),
-                        lhsT_scale=w2_scale[:, g * 2 * N + cols : g * 2 * N + cols + P],
+                        lhsT_scale=w2_scale[g][:, cols : cols + P],
                         rhs=h_codes[:, slots].bitcast(FP8X4),
                         rhs_scale=h_scale[:, slots],
                         start=True,
@@ -137,9 +139,16 @@ def tile_moe_dyn_none_kernel(
                     )
                 y_sb = keep.tile([P, PAIR], F32, name=f"y_sb{g}{c}")
                 nc.scalar.copy(y_sb[:], y[:])
+                staged[g, c] = y_sb
+        results = [
+            keep.tile([P, T], F32, align_bytes=64, name="result0"),
+            keep.tile([P, T], F32, align_bytes=64, name="result1"),
+        ]
+        for g in range(2):
+            for c in range(N // P):
                 nc.vector.tensor_tensor(
                     results[c][:].indirect(entries(tok, g * PAIR, PAIR)),
-                    y_sb[:],
+                    staged[g, c][:],
                     gates[:, g * PAIR : (g + 1) * PAIR],
                     mybir.AluOpType.mult,
                 )

@@ -60,7 +60,7 @@ def tile_moe_dyn_none_kernel(
         nc.vector.memset(w2_plane[:].bitcast(I32), 0)
 
         tok = load_list(nc, keep, offs, "tok")
-        nc.sync.dma_start(x_table[:, 0:T], words_in_hbm(x_words))
+        nc.scalar.dma_start(x_table[:, 0:T], words_in_hbm(x_words))
         col1 = load_list(nc, keep, offs2, "col1")
         col2 = load_list(nc, keep, offs3, "col2")
         load_scale_rows(nc.sync, w1_plane, w1_scales)
@@ -84,8 +84,8 @@ def tile_moe_dyn_none_kernel(
         gates = keep.tile([P, T], F32, align_bytes=64, tag="w1_plane_then_gates")
         nc.sync.dma_start(gates[:], gate)
 
-        w2_scale_first = keep.tile([P, 2 * N], U8, align_bytes=64)
-        nc.vector.tensor_copy(w2_scale_first[:], w2_plane[:].indirect(entries(col2, 0, 2 * N)))
+        w2_scale = keep.tile([P, B * N], U8, align_bytes=64)
+        nc.vector.tensor_copy(w2_scale[:], w2_plane[:].indirect(col2[:]))
 
         grouped = [keep.tile([P, PAIR * 4], BF16, align_bytes=64, name=f"grouped{g}", tag=f"grouped{g}") for g in range(2)]
         for m in range(B):
@@ -113,9 +113,6 @@ def tile_moe_dyn_none_kernel(
             half = grouped[m // 2][:].bitcast(F32)[:, (m % 2) * 2 * SLOTS : (m % 2 + 1) * 2 * SLOTS]
             nc.scalar.copy(half.rearrange("p (s u) -> p s u", u=2), turned[:].rearrange("p u s -> p s u"))
 
-        w2_scale_second = keep.tile([P, 2 * N], U8, align_bytes=64, tag="w1_codes1")
-        nc.vector.tensor_copy(w2_scale_second[:], w2_plane[:].indirect(entries(col2, 2 * N, 2 * N)))
-        w2_scale = [w2_scale_first, w2_scale_second]
         staged = {}
         for g in range(2):
             w2_codes = keep.tile([P, 2 * N], U32, align_bytes=64, name=f"w2_codes{g}", tag=("w1_codes0" if g == 0 else "rounded2"))
@@ -131,7 +128,7 @@ def tile_moe_dyn_none_kernel(
                     nc.tensor.matmul_mx(
                         out=y[:, slots],
                         lhsT=w2_codes[:, cols : cols + P].bitcast(FP8X4),
-                        lhsT_scale=w2_scale[g][:, cols : cols + P],
+                        lhsT_scale=w2_scale[:, g * 2 * N + cols : g * 2 * N + cols + P],
                         rhs=h_codes[:, slots].bitcast(FP8X4),
                         rhs_scale=h_scale[:, slots],
                         start=True,

@@ -18,7 +18,6 @@ P = 128
 SLOTS = 128
 PER_COL = 16
 X_WINDOW = 768
-PAIR = 2 * SLOTS
 
 
 def load_list(nc, pool, source, name):
@@ -48,7 +47,7 @@ def tile_moe_dyn_none_kernel(
     with ExitStack() as ctx:
         keep = ctx.enter_context(tc.tile_pool(name="keep", bufs=1))
         psum2 = ctx.enter_context(tc.psum_pool(name="psum2", bufs=2))
-        psum1 = ctx.enter_context(tc.psum_pool(name="psum1", bufs=1))
+        psum4 = ctx.enter_context(tc.psum_pool(name="psum4", bufs=4))
 
         w1_plane = keep.tile([P, E * H], U8, align_bytes=64, tag="w1_plane_then_gates")
         x_table = keep.tile([P, X_WINDOW], I32, align_bytes=64, tag="x_then_w1")
@@ -87,22 +86,26 @@ def tile_moe_dyn_none_kernel(
         w2_scale = keep.tile([P, B * N], U8, align_bytes=64)
         nc.vector.tensor_copy(w2_scale[:], w2_plane[:].indirect(col2[:]))
 
-        grouped = [keep.tile([P, PAIR * 4], BF16, align_bytes=64, name=f"grouped{g}", tag=f"grouped{g}") for g in range(2)]
+        w1_codes = []
+        for m in range(B):
+            codes = keep.tile([P, H], U32, align_bytes=64, name=f"w1_codes{m}", tag=f"w1_codes{m}")
+            nc.vector.tensor_copy(codes[:], w1_table[:].bitcast(U32).indirect(entries(col1, m * H, H)))
+            w1_codes.append(codes)
+
+        results = [keep.tile([P, T], F32, align_bytes=64, name=f"result{c}") for c in range(N // P)]
         for m in range(B):
             slots = slice(m * SLOTS, (m + 1) * SLOTS)
-            w1_codes = keep.tile([P, H], U32, align_bytes=64, name=f"w1_codes{m}", tag=f"w1_codes{m}")
-            nc.vector.tensor_copy(w1_codes[:], w1_table[:].bitcast(U32).indirect(entries(col1, m * H, H)))
-            h_t = psum2.tile([P, H], F32)
+            h_t = psum4.tile([P, H], F32)
             nc.tensor.matmul_mx(
                 out=h_t[:],
                 lhsT=x_codes[:, slots].bitcast(FP8X4),
                 lhsT_scale=x_scale[:, slots],
-                rhs=w1_codes[:].bitcast(FP8X4),
+                rhs=w1_codes[m][:].bitcast(FP8X4),
                 rhs_scale=w1_scale[:, m * H : (m + 1) * H],
                 start=True,
                 stop=True,
             )
-            rounded = keep.tile([P, H], BF16, align_bytes=64, name=f"rounded{m}", tag=f"rounded{m}")
+            rounded = keep.tile([P, H], BF16, align_bytes=64, name=f"rounded{m}")
             nc.scalar.copy(
                 rounded[:].rearrange("s (u p e) -> s u p e", u=2, e=2),
                 h_t[:].rearrange("s (p u e) -> s u p e", u=2, e=2),
@@ -110,43 +113,34 @@ def tile_moe_dyn_none_kernel(
             turned = psum2.tile([P, 2, SLOTS], F32)
             for u in range(2):
                 nc.tensor.transpose(turned[:, u, :], rounded[:].bitcast(F32)[:, u * P : (u + 1) * P], identity[:])
-            half = grouped[m // 2][:].bitcast(F32)[:, (m % 2) * 2 * SLOTS : (m % 2 + 1) * 2 * SLOTS]
-            nc.scalar.copy(half.rearrange("p (s u) -> p s u", u=2), turned[:].rearrange("p u s -> p s u"))
+            grouped = keep.tile([P, SLOTS * 4], BF16, align_bytes=64, name=f"grouped{m}", tag=f"grouped{m}")
+            nc.scalar.copy(grouped[:].bitcast(F32).rearrange("p (s u) -> p s u", u=2), turned[:].rearrange("p u s -> p s u"))
 
-        staged = {}
-        for g in range(2):
-            w2_codes = keep.tile([P, 2 * N], U32, align_bytes=64, name=f"w2_codes{g}", tag=("w1_codes0" if g == 0 else "rounded2"))
-            nc.vector.tensor_copy(w2_codes[:], w2_table[:].bitcast(U32).indirect(entries(col2, g * 2 * N, 2 * N)))
-            h_codes = keep.tile([P, PAIR], U32, align_bytes=64, name=f"h_codes{g}")
-            h_scale = keep.tile([P, PAIR], U8, align_bytes=64, name=f"h_scale{g}")
-            nc.vector.quantize_mx(out=h_codes[:].bitcast(FP8X4), scales=h_scale[:], in_=grouped[g][:])
+            if m % 2 == 0:
+                w2_codes = keep.tile([P, 2 * N], U32, align_bytes=64, name=f"w2_codes{m}", tag=("w1_codes0" if m == 0 else "grouped0"))
+                nc.vector.tensor_copy(w2_codes[:], w2_table[:].bitcast(U32).indirect(entries(col2, m * N, 2 * N)))
+            h_codes = keep.tile([P, SLOTS], U32, align_bytes=64, name=f"h_codes{m}")
+            h_scale = keep.tile([P, SLOTS], U8, align_bytes=64, name=f"h_scale{m}")
+            nc.vector.quantize_mx(out=h_codes[:].bitcast(FP8X4), scales=h_scale[:], in_=grouped[:])
+            y = psum2.tile([P, N // P, SLOTS], F32)
             for c in range(N // P):
-                y = psum1.tile([P, PAIR], F32, name=f"y{g}{c}")
-                for j in range(2):
-                    slots = slice(j * SLOTS, (j + 1) * SLOTS)
-                    cols = j * N + c * P
-                    nc.tensor.matmul_mx(
-                        out=y[:, slots],
-                        lhsT=w2_codes[:, cols : cols + P].bitcast(FP8X4),
-                        lhsT_scale=w2_scale[:, g * 2 * N + cols : g * 2 * N + cols + P],
-                        rhs=h_codes[:, slots].bitcast(FP8X4),
-                        rhs_scale=h_scale[:, slots],
-                        start=True,
-                        stop=True,
-                    )
-                y_sb = keep.tile([P, PAIR], F32, name=f"y_sb{g}{c}")
-                nc.scalar.copy(y_sb[:], y[:])
-                staged[g, c] = y_sb
-        results = [
-            keep.tile([P, T], F32, align_bytes=64, name="result0"),
-            keep.tile([P, T], F32, align_bytes=64, name="result1"),
-        ]
-        for g in range(2):
+                cols = (m % 2) * N + c * P
+                nc.tensor.matmul_mx(
+                    out=y[:, c, :],
+                    lhsT=w2_codes[:, cols : cols + P].bitcast(FP8X4),
+                    lhsT_scale=w2_scale[:, m * N + c * P : m * N + (c + 1) * P],
+                    rhs=h_codes[:].bitcast(FP8X4),
+                    rhs_scale=h_scale[:],
+                    start=True,
+                    stop=True,
+                )
+            y_sb = keep.tile([P, N // P, SLOTS], F32, name=f"y_sb{m}")
+            nc.scalar.copy(y_sb[:], y[:])
             for c in range(N // P):
                 nc.vector.tensor_tensor(
-                    results[c][:].indirect(entries(tok, g * PAIR, PAIR)),
-                    staged[g, c][:],
-                    gates[:, g * PAIR : (g + 1) * PAIR],
+                    results[c][:].indirect(entries(tok, m * SLOTS, SLOTS)),
+                    y_sb[:, c, :],
+                    gates[:, slots],
                     mybir.AluOpType.mult,
                 )
         for c in range(N // P):

@@ -49,40 +49,38 @@ def tile_moe_dyn_none_kernel(
         psum2 = ctx.enter_context(tc.psum_pool(name="psum2", bufs=2))
         psum4 = ctx.enter_context(tc.psum_pool(name="psum4", bufs=4))
 
-        w1_plane = keep.tile([P, E * H], U8, align_bytes=64, tag="w1_plane_then_gates")
-        x_table = keep.tile([P, X_WINDOW], I32, align_bytes=64, tag="x_then_w1")
-        x_plane = keep.tile([P, X_WINDOW], U8, align_bytes=64, tag="x_plane_then_w2")
+        x_plane = keep.tile([P, X_WINDOW], U8, align_bytes=64)
+        w1_plane = keep.tile([P, E * H], U8, align_bytes=64)
+        x_table = keep.tile([P, X_WINDOW], I32, align_bytes=64)
         w2_plane = keep.tile([P, E * N], U8, align_bytes=64)
-        nc.vector.memset(w1_plane[:].bitcast(I32), 0)
-        nc.vector.memset(x_table[:, T:X_WINDOW], 0)
         nc.vector.memset(x_plane[:].bitcast(I32), 0)
+        nc.vector.memset(w1_plane[:].bitcast(I32), 0)
         nc.vector.memset(w2_plane[:].bitcast(I32), 0)
+        nc.vector.memset(x_table[:, T:X_WINDOW], 0)
 
         tok = load_list(nc, keep, offs, "tok")
-        nc.scalar.dma_start(x_table[:, 0:T], words_in_hbm(x_words))
         col1 = load_list(nc, keep, offs2, "col1")
         col2 = load_list(nc, keep, offs3, "col2")
-        load_scale_rows(nc.sync, w1_plane, w1_scales)
+        nc.sync.dma_start(x_table[:, 0:T], words_in_hbm(x_words))
         load_scale_rows(nc.sync, x_plane, x_scales)
+        load_scale_rows(nc.sync, w1_plane, w1_scales)
         load_scale_rows(nc.sync, w2_plane, w2_scales)
+        w1_table = keep.tile([P, E * H], I32, align_bytes=64)
+        nc.sync.dma_start(w1_table[:], words_in_hbm(w1_words))
+        w2_table = keep.tile([P, E * N], I32, align_bytes=64)
+        nc.sync.dma_start(w2_table[:], words_in_hbm(w2_words))
+        gates = keep.tile([P, T], F32, align_bytes=64)
+        nc.sync.dma_start(gates[:], gate)
 
         identity = keep.tile([P, P], F32)
         make_identity(nc, identity[:])
 
         x_codes = keep.tile([P, T], U32, align_bytes=64)
         nc.vector.tensor_copy(x_codes[:], x_table[:].bitcast(U32).indirect(tok[:]))
-        w1_table = keep.tile([P, E * H], I32, align_bytes=64, tag="x_then_w1")
-        nc.sync.dma_start(w1_table[:], words_in_hbm(w1_words))
-
-        w1_scale = keep.tile([P, B * H], U8, align_bytes=64)
-        nc.vector.tensor_copy(w1_scale[:], w1_plane[:].indirect(col1[:]))
         x_scale = keep.tile([P, T], U8, align_bytes=64)
         nc.vector.tensor_copy(x_scale[:], x_plane[:].indirect(tok[:]))
-        w2_table = keep.tile([P, E * N], I32, align_bytes=64, tag="x_plane_then_w2")
-        nc.sync.dma_start(w2_table[:], words_in_hbm(w2_words))
-        gates = keep.tile([P, T], F32, align_bytes=64, tag="w1_plane_then_gates")
-        nc.sync.dma_start(gates[:], gate)
-
+        w1_scale = keep.tile([P, B * H], U8, align_bytes=64)
+        nc.vector.tensor_copy(w1_scale[:], w1_plane[:].indirect(col1[:]))
         w2_scale = keep.tile([P, B * N], U8, align_bytes=64)
         nc.vector.tensor_copy(w2_scale[:], w2_plane[:].indirect(col2[:]))
 

@@ -18,6 +18,7 @@ P = 128
 SLOTS = 128
 PER_COL = 16
 X_WINDOW = 768
+ROWS_AT = 16
 
 
 def load_list(nc, pool, source, name):
@@ -40,6 +41,11 @@ def load_scale_rows(queue, plane, scales):
         queue.dma_start(plane[r:P:32, 0:width].bitcast(I32), scales[0, r:16:4, :].bitcast(I32))
 
 
+def lay_scale_rows(nc, plane, rows):
+    for r in range(4):
+        nc.sync.dma_start(plane[r:P:32, :].bitcast(I32), rows[ROWS_AT + r : ROWS_AT + 16 : 4, :].bitcast(I32))
+
+
 def tile_moe_dyn_none_kernel(
     tc, x_words, x_scales, w1_words, w1_scales, w2_words, w2_scales, gate, offs, offs2, offs3, out
 ):
@@ -49,10 +55,10 @@ def tile_moe_dyn_none_kernel(
         psum2 = ctx.enter_context(tc.psum_pool(name="psum2", bufs=2))
         psum4 = ctx.enter_context(tc.psum_pool(name="psum4", bufs=4))
 
-        x_plane = keep.tile([P, X_WINDOW], U8, align_bytes=64)
+        x_plane = keep.tile([P, X_WINDOW], U8, align_bytes=64, tag="x_plane_then_w2")
         w1_plane = keep.tile([P, E * H], U8, align_bytes=64)
         x_table = keep.tile([P, X_WINDOW], I32, align_bytes=64)
-        w2_plane = keep.tile([P, E * N], U8, align_bytes=64)
+        w2_plane = keep.tile([P, E * N], U8, align_bytes=64, tag="w2_plane_then_gates")
         nc.vector.memset(x_plane[:].bitcast(I32), 0)
         nc.vector.memset(w1_plane[:].bitcast(I32), 0)
         nc.vector.memset(w2_plane[:].bitcast(I32), 0)
@@ -62,27 +68,31 @@ def tile_moe_dyn_none_kernel(
         col1 = load_list(nc, keep, offs2, "col1")
         col2 = load_list(nc, keep, offs3, "col2")
         nc.sync.dma_start(x_table[:, 0:T], words_in_hbm(x_words))
-        load_scale_rows(nc.sync, x_plane, x_scales)
+        nc.sync.dma_start(x_plane[ROWS_AT : ROWS_AT + 16, 0:T].bitcast(I32), x_scales[0].bitcast(I32))
         load_scale_rows(nc.sync, w1_plane, w1_scales)
-        load_scale_rows(nc.sync, w2_plane, w2_scales)
+        nc.sync.dma_start(w2_plane[ROWS_AT : ROWS_AT + 16, :].bitcast(I32), w2_scales[0].bitcast(I32))
         w1_table = keep.tile([P, E * H], I32, align_bytes=64)
         nc.sync.dma_start(w1_table[:], words_in_hbm(w1_words))
-        w2_table = keep.tile([P, E * N], I32, align_bytes=64)
-        nc.sync.dma_start(w2_table[:], words_in_hbm(w2_words))
-        gates = keep.tile([P, T], F32, align_bytes=64)
-        nc.sync.dma_start(gates[:], gate)
 
         identity = keep.tile([P, P], F32)
         make_identity(nc, identity[:])
 
         x_codes = keep.tile([P, T], U32, align_bytes=64)
         nc.vector.tensor_copy(x_codes[:], x_table[:].bitcast(U32).indirect(tok[:]))
+        x_rows = keep.tile([P, T], U8, align_bytes=64)
+        nc.vector.tensor_copy(x_rows[:], x_plane[:].indirect(tok[:]))
         x_scale = keep.tile([P, T], U8, align_bytes=64)
-        nc.vector.tensor_copy(x_scale[:], x_plane[:].indirect(tok[:]))
+        lay_scale_rows(nc, x_scale, x_rows)
+        w2_table = keep.tile([P, E * N], I32, align_bytes=64, tag="x_plane_then_w2")
+        nc.sync.dma_start(w2_table[:], words_in_hbm(w2_words))
         w1_scale = keep.tile([P, B * H], U8, align_bytes=64)
         nc.vector.tensor_copy(w1_scale[:], w1_plane[:].indirect(col1[:]))
+        w2_rows = keep.tile([P, B * N], U8, align_bytes=64)
+        nc.vector.tensor_copy(w2_rows[:], w2_plane[:].indirect(col2[:]))
         w2_scale = keep.tile([P, B * N], U8, align_bytes=64)
-        nc.vector.tensor_copy(w2_scale[:], w2_plane[:].indirect(col2[:]))
+        lay_scale_rows(nc, w2_scale, w2_rows)
+        gates = keep.tile([P, T], F32, align_bytes=64, tag="w2_plane_then_gates")
+        nc.sync.dma_start(gates[:], gate)
 
         w1_codes = []
         for m in range(B):

@@ -58,7 +58,7 @@ def tile_moe_dyn_none_kernel(
         x_plane = keep.tile([P, X_WINDOW], U8, align_bytes=64, tag="x_plane_then_w2")
         w1_plane = keep.tile([P, E * H], U8, align_bytes=64)
         x_table = keep.tile([P, X_WINDOW], I32, align_bytes=64)
-        w2_plane = keep.tile([P, E * N], U8, align_bytes=64, tag="w2_plane_then_gates")
+        w2_plane = keep.tile([P, E * N], U8, align_bytes=64)
         nc.vector.memset(x_plane[:].bitcast(I32), 0)
         nc.vector.memset(w1_plane[:].bitcast(I32), 0)
         nc.vector.memset(w2_plane[:].bitcast(I32), 0)
@@ -70,7 +70,10 @@ def tile_moe_dyn_none_kernel(
         nc.sync.dma_start(x_table[:, 0:T], words_in_hbm(x_words))
         nc.sync.dma_start(x_plane[ROWS_AT : ROWS_AT + 16, 0:T].bitcast(I32), x_scales[0].bitcast(I32))
         load_scale_rows(nc.sync, w1_plane, w1_scales)
-        nc.sync.dma_start(w2_plane[ROWS_AT : ROWS_AT + 16, :].bitcast(I32), w2_scales[0].bitcast(I32))
+        for half in range(2):
+            nc.sync.dma_start(
+                w2_plane[64 * half : 64 * half + 8, :].bitcast(I32), w2_scales[0, 8 * half : 8 * half + 8, :].bitcast(I32)
+            )
         w1_table = keep.tile([P, E * H], I32, align_bytes=64)
         nc.sync.dma_start(w1_table[:], words_in_hbm(w1_words))
 
@@ -89,10 +92,6 @@ def tile_moe_dyn_none_kernel(
         nc.vector.tensor_copy(w1_scale[:], w1_plane[:].indirect(col1[:]))
         w2_rows = keep.tile([P, B * N], U8, align_bytes=64)
         nc.vector.tensor_copy(w2_rows[:], w2_plane[:].indirect(col2[:]))
-        w2_scale = keep.tile([P, B * N], U8, align_bytes=64)
-        lay_scale_rows(nc, w2_scale, w2_rows)
-        gates = keep.tile([P, T], F32, align_bytes=64, tag="w2_plane_then_gates")
-        nc.sync.dma_start(gates[:], gate)
 
         w1_codes = []
         for m in range(B):
@@ -103,38 +102,49 @@ def tile_moe_dyn_none_kernel(
         results = [keep.tile([P, T], F32, align_bytes=64, name=f"result{c}") for c in range(N // P)]
         for m in range(B):
             slots = slice(m * SLOTS, (m + 1) * SLOTS)
-            h_t = psum4.tile([P, H], F32)
-            nc.tensor.matmul_mx(
-                out=h_t[:],
-                lhsT=x_codes[:, slots].bitcast(FP8X4),
-                lhsT_scale=x_scale[:, slots],
-                rhs=w1_codes[m][:].bitcast(FP8X4),
-                rhs_scale=w1_scale[:, m * H : (m + 1) * H],
-                start=True,
-                stop=True,
-            )
             rounded = keep.tile([P, H], BF16, align_bytes=64, name=f"rounded{m}")
-            nc.scalar.copy(
-                rounded[:].rearrange("s (u p e) -> s u p e", u=2, e=2),
-                h_t[:].rearrange("s (p u e) -> s u p e", u=2, e=2),
-            )
+            parts = 2 if m == 0 else 1
+            width = H // parts
+            for part in range(parts):
+                h_t = psum4.tile([P, width], F32)
+                nc.tensor.matmul_mx(
+                    out=h_t[:],
+                    lhsT=x_codes[:, slots].bitcast(FP8X4),
+                    lhsT_scale=x_scale[:, slots],
+                    rhs=w1_codes[m][:, part * width : (part + 1) * width].bitcast(FP8X4),
+                    rhs_scale=w1_scale[:, m * H + part * width : m * H + (part + 1) * width],
+                    start=True,
+                    stop=True,
+                )
+                nc.scalar.copy(
+                    rounded[:].rearrange("s (u p e) -> s u p e", u=2, e=2)[:, :, part * width // 4 : (part + 1) * width // 4, :],
+                    h_t[:].rearrange("s (p u e) -> s u p e", u=2, e=2),
+                )
             turned = psum2.tile([P, 2, SLOTS], F32)
             for u in range(2):
                 nc.tensor.transpose(turned[:, u, :], rounded[:].bitcast(F32)[:, u * P : (u + 1) * P], identity[:])
             grouped = keep.tile([P, SLOTS * 4], BF16, align_bytes=64, name=f"grouped{m}", tag=f"grouped{m}")
             nc.scalar.copy(grouped[:].bitcast(F32).rearrange("p (s u) -> p s u", u=2), turned[:].rearrange("p u s -> p s u"))
 
+            if m == 0:
+                w2_scale = keep.tile([P, B * N], U8, align_bytes=64, tag="w1_codes0")
+                for half in range(2):
+                    low = 64 * half
+                    nc.sync.dma_start(w2_scale[low + 32 : low + 36, :].bitcast(I32), w2_rows[low + 4 : low + 8, :].bitcast(I32))
+                    nc.vector.tensor_copy(w2_scale[low : low + 32, :].bitcast(I32), w2_rows[low : low + 32, :].bitcast(I32))
+                gates = keep.tile([P, T], F32, align_bytes=64, tag="w1_codes1")
+                nc.sync.dma_start(gates[:], gate)
             if m % 2 == 0:
-                w2_codes = keep.tile([P, 2 * N], U32, align_bytes=64, name=f"w2_codes{m}", tag=("w1_codes0" if m == 0 else "grouped0"))
+                w2_codes = keep.tile([P, 2 * N], U32, align_bytes=64, name=f"w2_codes{m}", tag=("w2_codes0" if m == 0 else "grouped0"))
                 nc.vector.tensor_copy(w2_codes[:], w2_table[:].bitcast(U32).indirect(entries(col2, m * N, 2 * N)))
             h_codes = keep.tile([P, SLOTS], U32, align_bytes=64, name=f"h_codes{m}")
             h_scale = keep.tile([P, SLOTS], U8, align_bytes=64, name=f"h_scale{m}")
             nc.vector.quantize_mx(out=h_codes[:].bitcast(FP8X4), scales=h_scale[:], in_=grouped[:])
-            y = psum2.tile([P, N // P, SLOTS], F32)
             for c in range(N // P):
                 cols = (m % 2) * N + c * P
+                y = psum2.tile([P, SLOTS], F32)
                 nc.tensor.matmul_mx(
-                    out=y[:, c, :],
+                    out=y[:],
                     lhsT=w2_codes[:, cols : cols + P].bitcast(FP8X4),
                     lhsT_scale=w2_scale[:, m * N + c * P : m * N + (c + 1) * P],
                     rhs=h_codes[:].bitcast(FP8X4),
@@ -142,12 +152,11 @@ def tile_moe_dyn_none_kernel(
                     start=True,
                     stop=True,
                 )
-            y_sb = keep.tile([P, N // P, SLOTS], F32, name=f"y_sb{m}")
-            nc.scalar.copy(y_sb[:], y[:])
-            for c in range(N // P):
+                y_sb = keep.tile([P, SLOTS], F32, name=f"y_sb{m}{c}")
+                nc.scalar.copy(y_sb[:], y[:])
                 nc.vector.tensor_tensor(
                     results[c][:].indirect(entries(tok, m * SLOTS, SLOTS)),
-                    y_sb[:, c, :],
+                    y_sb[:],
                     gates[:, slots],
                     mybir.AluOpType.mult,
                 )

@@ -18,7 +18,7 @@ P = 128
 SLOTS = 128
 PER_COL = 16
 X_WINDOW = 768
-ROWS_AT = 16
+ROW_STEP = 8
 
 
 def load_list(nc, pool, source, name):
@@ -35,15 +35,18 @@ def words_in_hbm(words):
     return words[0].rearrange("p c d -> p (c d)").bitcast(I32)
 
 
-def load_scale_rows(queue, plane, scales):
-    width = scales.shape[2]
-    for r in range(4):
-        queue.dma_start(plane[r:P:32, 0:width].bitcast(I32), scales[0, r:16:4, :].bitcast(I32))
+def load_scale_rows(nc, plane, scales):
+    nc.sync.dma_start(plane[0:P:ROW_STEP, 0 : scales.shape[2]].bitcast(I32), scales[0].bitcast(I32))
 
 
-def lay_scale_rows(nc, plane, rows):
+def gather_scales(nc, pool, plane, offsets, name):
+    count = offsets.shape[1] * PER_COL
+    rows = pool.tile([P, count], U8, align_bytes=64, name=f"{name}_rows")
+    nc.vector.tensor_copy(rows[:], plane[:].indirect(offsets[:]))
+    laid = pool.tile([P, count], U8, align_bytes=64, name=f"{name}_scale")
     for r in range(4):
-        nc.sync.dma_start(plane[r:P:32, :].bitcast(I32), rows[ROWS_AT + r : ROWS_AT + 16 : 4, :].bitcast(I32))
+        nc.sync.dma_start(laid[r:P:32, :].bitcast(I32), rows[ROW_STEP * r : P : 32, :].bitcast(I32))
+    return laid
 
 
 def tile_moe_dyn_none_kernel(
@@ -52,46 +55,39 @@ def tile_moe_dyn_none_kernel(
     nc = tc.nc
     with ExitStack() as ctx:
         keep = ctx.enter_context(tc.tile_pool(name="keep", bufs=1))
-        psum2 = ctx.enter_context(tc.psum_pool(name="psum2", bufs=2))
-        psum4 = ctx.enter_context(tc.psum_pool(name="psum4", bufs=4))
+        psum = ctx.enter_context(tc.psum_pool(name="psum", bufs=1))
 
-        x_plane = keep.tile([P, X_WINDOW], U8, align_bytes=64, tag="x_plane_then_w2")
-        w1_plane = keep.tile([P, E * H], U8, align_bytes=64)
+        x_plane = keep.tile([P, X_WINDOW], U8, align_bytes=64)
+        w1_plane = keep.tile([P, E * H], U8, align_bytes=64, tag="w1_plane_then_w2_table")
+        w2_plane = keep.tile([P, E * N], U8, align_bytes=64, tag="w2_plane_then_gates")
         x_table = keep.tile([P, X_WINDOW], I32, align_bytes=64)
-        w2_plane = keep.tile([P, E * N], U8, align_bytes=64)
         nc.vector.memset(x_plane[:].bitcast(I32), 0)
         nc.vector.memset(w1_plane[:].bitcast(I32), 0)
         nc.vector.memset(w2_plane[:].bitcast(I32), 0)
         nc.vector.memset(x_table[:, T:X_WINDOW], 0)
 
         tok = load_list(nc, keep, offs, "tok")
+        load_scale_rows(nc, x_plane, x_scales)
         col1 = load_list(nc, keep, offs2, "col1")
-        col2 = load_list(nc, keep, offs3, "col2")
+        load_scale_rows(nc, w1_plane, w1_scales)
         nc.sync.dma_start(x_table[:, 0:T], words_in_hbm(x_words))
-        nc.sync.dma_start(x_plane[ROWS_AT : ROWS_AT + 16, 0:T].bitcast(I32), x_scales[0].bitcast(I32))
-        load_scale_rows(nc.sync, w1_plane, w1_scales)
-        for half in range(2):
-            nc.sync.dma_start(
-                w2_plane[64 * half : 64 * half + 8, :].bitcast(I32), w2_scales[0, 8 * half : 8 * half + 8, :].bitcast(I32)
-            )
+        col2 = load_list(nc, keep, offs3, "col2")
+        load_scale_rows(nc, w2_plane, w2_scales)
         w1_table = keep.tile([P, E * H], I32, align_bytes=64)
         nc.sync.dma_start(w1_table[:], words_in_hbm(w1_words))
 
         identity = keep.tile([P, P], F32)
         make_identity(nc, identity[:])
 
+        x_scale = gather_scales(nc, keep, x_plane, tok, "x")
+        w1_scale = gather_scales(nc, keep, w1_plane, col1, "w1")
+        w2_table = keep.tile([P, E * N], I32, align_bytes=64, tag="w1_plane_then_w2_table")
+        nc.sync.dma_start(w2_table[:], words_in_hbm(w2_words))
         x_codes = keep.tile([P, T], U32, align_bytes=64)
         nc.vector.tensor_copy(x_codes[:], x_table[:].bitcast(U32).indirect(tok[:]))
-        x_rows = keep.tile([P, T], U8, align_bytes=64)
-        nc.vector.tensor_copy(x_rows[:], x_plane[:].indirect(tok[:]))
-        x_scale = keep.tile([P, T], U8, align_bytes=64)
-        lay_scale_rows(nc, x_scale, x_rows)
-        w2_table = keep.tile([P, E * N], I32, align_bytes=64, tag="x_plane_then_w2")
-        nc.sync.dma_start(w2_table[:], words_in_hbm(w2_words))
-        w1_scale = keep.tile([P, B * H], U8, align_bytes=64)
-        nc.vector.tensor_copy(w1_scale[:], w1_plane[:].indirect(col1[:]))
-        w2_rows = keep.tile([P, B * N], U8, align_bytes=64)
-        nc.vector.tensor_copy(w2_rows[:], w2_plane[:].indirect(col2[:]))
+        w2_scale = gather_scales(nc, keep, w2_plane, col2, "w2")
+        gates = keep.tile([P, T], F32, align_bytes=64, tag="w2_plane_then_gates")
+        nc.sync.dma_start(gates[:], gate)
 
         w1_codes = []
         for m in range(B):
@@ -100,13 +96,16 @@ def tile_moe_dyn_none_kernel(
             w1_codes.append(codes)
 
         results = [keep.tile([P, T], F32, align_bytes=64, name=f"result{c}") for c in range(N // P)]
-        for m in range(B):
+        rounded, grouped, quantised, w2_codes = {}, {}, {}, {}
+
+        def first_product(m):
             slots = slice(m * SLOTS, (m + 1) * SLOTS)
-            rounded = keep.tile([P, H], BF16, align_bytes=64, name=f"rounded{m}")
+            rounded[m] = keep.tile([P, H], BF16, align_bytes=64, name=f"rounded{m}", tag=f"rounded{m}")
             parts = 2 if m == 0 else 1
             width = H // parts
             for part in range(parts):
-                h_t = psum4.tile([P, width], F32)
+                bank = "h_first" if parts == 2 and part == 0 else f"h{m % 2}"
+                h_t = psum.tile([P, width], F32, name=f"h_t{m}{part}", tag=bank)
                 nc.tensor.matmul_mx(
                     out=h_t[:],
                     lhsT=x_codes[:, slots].bitcast(FP8X4),
@@ -117,48 +116,70 @@ def tile_moe_dyn_none_kernel(
                     stop=True,
                 )
                 nc.scalar.copy(
-                    rounded[:].rearrange("s (u p e) -> s u p e", u=2, e=2)[:, :, part * width // 4 : (part + 1) * width // 4, :],
+                    rounded[m][:].rearrange("s (u p e) -> s u p e", u=2, e=2)[:, :, part * width // 4 : (part + 1) * width // 4, :],
                     h_t[:].rearrange("s (p u e) -> s u p e", u=2, e=2),
                 )
-            turned = psum2.tile([P, 2, SLOTS], F32)
-            for u in range(2):
-                nc.tensor.transpose(turned[:, u, :], rounded[:].bitcast(F32)[:, u * P : (u + 1) * P], identity[:])
-            grouped = keep.tile([P, SLOTS * 4], BF16, align_bytes=64, name=f"grouped{m}", tag=f"grouped{m}")
-            nc.scalar.copy(grouped[:].bitcast(F32).rearrange("p (s u) -> p s u", u=2), turned[:].rearrange("p u s -> p s u"))
 
-            if m == 0:
-                w2_scale = keep.tile([P, B * N], U8, align_bytes=64, tag="w1_codes0")
-                for half in range(2):
-                    low = 64 * half
-                    nc.sync.dma_start(w2_scale[low + 32 : low + 36, :].bitcast(I32), w2_rows[low + 4 : low + 8, :].bitcast(I32))
-                    nc.vector.tensor_copy(w2_scale[low : low + 32, :].bitcast(I32), w2_rows[low : low + 32, :].bitcast(I32))
-                gates = keep.tile([P, T], F32, align_bytes=64, tag="w1_codes1")
-                nc.sync.dma_start(gates[:], gate)
-            if m % 2 == 0:
-                w2_codes = keep.tile([P, 2 * N], U32, align_bytes=64, name=f"w2_codes{m}", tag=("w2_codes0" if m == 0 else "grouped0"))
-                nc.vector.tensor_copy(w2_codes[:], w2_table[:].bitcast(U32).indirect(entries(col2, m * N, 2 * N)))
+        def turn(m):
+            turned = psum.tile([P, 2, SLOTS], F32, name=f"turned{m}", tag=(f"t{m}" if m < 2 else f"y{m - 2}"))
+            for u in range(2):
+                nc.tensor.transpose(turned[:, u, :], rounded[m][:].bitcast(F32)[:, u * P : (u + 1) * P], identity[:])
+            grouped[m] = keep.tile([P, SLOTS * 4], BF16, align_bytes=64, name=f"grouped{m}")
+            nc.scalar.copy(grouped[m][:].bitcast(F32).rearrange("p (s u) -> p s u", u=2), turned[:].rearrange("p u s -> p s u"))
+
+        def quantise(m):
             h_codes = keep.tile([P, SLOTS], U32, align_bytes=64, name=f"h_codes{m}")
             h_scale = keep.tile([P, SLOTS], U8, align_bytes=64, name=f"h_scale{m}")
-            nc.vector.quantize_mx(out=h_codes[:].bitcast(FP8X4), scales=h_scale[:], in_=grouped[:])
+            nc.vector.quantize_mx(out=h_codes[:].bitcast(FP8X4), scales=h_scale[:], in_=grouped[m][:])
+            quantised[m] = (h_codes, h_scale)
+
+        def gather_w2_words(pair):
+            tag = "w2_codes0" if pair == 0 else "w1_codes3"
+            w2_codes[pair] = keep.tile([P, 2 * N], U32, align_bytes=64, name=f"w2_codes{pair}", tag=tag)
+            nc.vector.tensor_copy(w2_codes[pair][:], w2_table[:].bitcast(U32).indirect(entries(col2, pair * 2 * N, 2 * N)))
+
+        def second_product(m):
+            slots = slice(m * SLOTS, (m + 1) * SLOTS)
+            h_codes, h_scale = quantised[m]
+            y = psum.tile([P, N // P, SLOTS], F32, name=f"y{m}", tag=(f"y{m}" if m < 2 else f"t{m - 2}"))
             for c in range(N // P):
-                cols = (m % 2) * N + c * P
-                y = psum2.tile([P, SLOTS], F32)
+                cols = slice((m % 2) * N + c * P, (m % 2) * N + (c + 1) * P)
                 nc.tensor.matmul_mx(
-                    out=y[:],
-                    lhsT=w2_codes[:, cols : cols + P].bitcast(FP8X4),
+                    out=y[:, c, :],
+                    lhsT=w2_codes[m // 2][:, cols].bitcast(FP8X4),
                     lhsT_scale=w2_scale[:, m * N + c * P : m * N + (c + 1) * P],
                     rhs=h_codes[:].bitcast(FP8X4),
                     rhs_scale=h_scale[:],
                     start=True,
                     stop=True,
                 )
-                y_sb = keep.tile([P, SLOTS], F32, name=f"y_sb{m}{c}")
-                nc.scalar.copy(y_sb[:], y[:])
+            y_sb = keep.tile([P, N // P, SLOTS], F32, name=f"y_sb{m}")
+            nc.scalar.copy(y_sb[:], y[:])
+            for c in range(N // P):
                 nc.vector.tensor_tensor(
                     results[c][:].indirect(entries(tok, m * SLOTS, SLOTS)),
-                    y_sb[:],
+                    y_sb[:, c, :],
                     gates[:, slots],
                     mybir.AluOpType.mult,
                 )
+
+        first_product(0)
+        first_product(1)
+        turn(0)
+        gather_w2_words(0)
+        quantise(0)
+        turn(1)
+        first_product(2)
+        quantise(1)
+        second_product(0)
+        first_product(3)
+        gather_w2_words(1)
+        turn(2)
+        quantise(2)
+        second_product(1)
+        turn(3)
+        quantise(3)
+        second_product(2)
+        second_product(3)
         for c in range(N // P):
             nc.sync.dma_start(out[c * P : (c + 1) * P, :], results[c][:])

@@ -19,6 +19,9 @@ SLOTS = 128
 PER_COL = 16
 X_WINDOW = 768
 ROW_STEP = 8
+H_BANKS = (("a", "b"), ("c",), ("b",), ("f",))
+TURN_BANKS = ("d", "e", "a", "c")
+Y_BANKS = (("f", "g"), ("a",), ("c",), ("d",))
 
 
 def load_list(nc, pool, source, name):
@@ -57,8 +60,8 @@ def tile_moe_dyn_none_kernel(
         keep = ctx.enter_context(tc.tile_pool(name="keep", bufs=1))
         psum = ctx.enter_context(tc.psum_pool(name="psum", bufs=1))
 
-        x_plane = keep.tile([P, X_WINDOW], U8, align_bytes=64)
-        w1_plane = keep.tile([P, E * H], U8, align_bytes=64, tag="w1_plane_then_w2_table")
+        x_plane = keep.tile([P, X_WINDOW], U8, align_bytes=64, tag="x_plane_then_w2_table")
+        w1_plane = keep.tile([P, E * H], U8, align_bytes=64)
         w2_plane = keep.tile([P, E * N], U8, align_bytes=64, tag="w2_plane_then_gates")
         x_table = keep.tile([P, X_WINDOW], I32, align_bytes=64)
         nc.vector.memset(x_plane[:].bitcast(I32), 0)
@@ -67,11 +70,12 @@ def tile_moe_dyn_none_kernel(
         nc.vector.memset(x_table[:, T:X_WINDOW], 0)
 
         tok = load_list(nc, keep, offs, "tok")
-        load_scale_rows(nc, x_plane, x_scales)
         col1 = load_list(nc, keep, offs2, "col1")
-        load_scale_rows(nc, w1_plane, w1_scales)
-        nc.sync.dma_start(x_table[:, 0:T], words_in_hbm(x_words))
         col2 = load_list(nc, keep, offs3, "col2")
+        load_scale_rows(nc, x_plane, x_scales)
+        nc.sync.dma_start(x_table[:, 0:T], words_in_hbm(x_words))
+        for r in range(4):
+            nc.sync.dma_start(w1_plane[r:P:32, :].bitcast(I32), w1_scales[0, r:16:4, :].bitcast(I32))
         load_scale_rows(nc, w2_plane, w2_scales)
         w1_table = keep.tile([P, E * H], I32, align_bytes=64)
         nc.sync.dma_start(w1_table[:], words_in_hbm(w1_words))
@@ -80,11 +84,12 @@ def tile_moe_dyn_none_kernel(
         make_identity(nc, identity[:])
 
         x_scale = gather_scales(nc, keep, x_plane, tok, "x")
-        w1_scale = gather_scales(nc, keep, w1_plane, col1, "w1")
-        w2_table = keep.tile([P, E * N], I32, align_bytes=64, tag="w1_plane_then_w2_table")
+        w2_table = keep.tile([P, E * N], I32, align_bytes=64, tag="x_plane_then_w2_table")
         nc.sync.dma_start(w2_table[:], words_in_hbm(w2_words))
         x_codes = keep.tile([P, T], U32, align_bytes=64)
         nc.vector.tensor_copy(x_codes[:], x_table[:].bitcast(U32).indirect(tok[:]))
+        w1_scale = keep.tile([P, B * H], U8, align_bytes=64)
+        nc.vector.tensor_copy(w1_scale[:], w1_plane[:].indirect(col1[:]))
         w2_scale = gather_scales(nc, keep, w2_plane, col2, "w2")
         gates = keep.tile([P, T], F32, align_bytes=64, tag="w2_plane_then_gates")
         nc.sync.dma_start(gates[:], gate)
@@ -104,7 +109,7 @@ def tile_moe_dyn_none_kernel(
             parts = 2 if m == 0 else 1
             width = H // parts
             for part in range(parts):
-                bank = "h_first" if parts == 2 and part == 0 else f"h{m % 2}"
+                bank = H_BANKS[m][part]
                 h_t = psum.tile([P, width], F32, name=f"h_t{m}{part}", tag=bank)
                 nc.tensor.matmul_mx(
                     out=h_t[:],
@@ -121,40 +126,43 @@ def tile_moe_dyn_none_kernel(
                 )
 
         def turn(m):
-            turned = psum.tile([P, 2, SLOTS], F32, name=f"turned{m}", tag=(f"t{m}" if m < 2 else f"y{m - 2}"))
+            turned = psum.tile([P, 2, SLOTS], F32, name=f"turned{m}", tag=TURN_BANKS[m])
             for u in range(2):
                 nc.tensor.transpose(turned[:, u, :], rounded[m][:].bitcast(F32)[:, u * P : (u + 1) * P], identity[:])
-            grouped[m] = keep.tile([P, SLOTS * 4], BF16, align_bytes=64, name=f"grouped{m}")
+            grouped[m] = keep.tile([P, SLOTS * 4], BF16, align_bytes=64, name=f"grouped{m}", tag=(f"grouped{m}" if m < 2 else f"h_codes{m - 2}"))
             nc.scalar.copy(grouped[m][:].bitcast(F32).rearrange("p (s u) -> p s u", u=2), turned[:].rearrange("p u s -> p s u"))
 
         def quantise(m):
-            h_codes = keep.tile([P, SLOTS], U32, align_bytes=64, name=f"h_codes{m}")
+            h_codes = keep.tile([P, SLOTS], U32, align_bytes=64, name=f"h_codes{m}", tag=f"h_codes{m}")
             h_scale = keep.tile([P, SLOTS], U8, align_bytes=64, name=f"h_scale{m}")
             nc.vector.quantize_mx(out=h_codes[:].bitcast(FP8X4), scales=h_scale[:], in_=grouped[m][:])
             quantised[m] = (h_codes, h_scale)
 
         def gather_w2_words(pair):
-            tag = "w2_codes0" if pair == 0 else "w1_codes3"
+            tag = "w2_codes0" if pair == 0 else "grouped0"
             w2_codes[pair] = keep.tile([P, 2 * N], U32, align_bytes=64, name=f"w2_codes{pair}", tag=tag)
             nc.vector.tensor_copy(w2_codes[pair][:], w2_table[:].bitcast(U32).indirect(entries(col2, pair * 2 * N, 2 * N)))
 
         def second_product(m):
             slots = slice(m * SLOTS, (m + 1) * SLOTS)
             h_codes, h_scale = quantised[m]
-            y = psum.tile([P, N // P, SLOTS], F32, name=f"y{m}", tag=(f"y{m}" if m < 2 else f"t{m - 2}"))
-            for c in range(N // P):
-                cols = slice((m % 2) * N + c * P, (m % 2) * N + (c + 1) * P)
-                nc.tensor.matmul_mx(
-                    out=y[:, c, :],
-                    lhsT=w2_codes[m // 2][:, cols].bitcast(FP8X4),
-                    lhsT_scale=w2_scale[:, m * N + c * P : m * N + (c + 1) * P],
-                    rhs=h_codes[:].bitcast(FP8X4),
-                    rhs_scale=h_scale[:],
-                    start=True,
-                    stop=True,
-                )
             y_sb = keep.tile([P, N // P, SLOTS], F32, name=f"y_sb{m}")
-            nc.scalar.copy(y_sb[:], y[:])
+            halves = N // P // len(Y_BANKS[m])
+            for b, bank in enumerate(Y_BANKS[m]):
+                y = psum.tile([P, halves, SLOTS], F32, name=f"y{m}{b}", tag=bank)
+                for j in range(halves):
+                    c = b * halves + j
+                    cols = slice((m % 2) * N + c * P, (m % 2) * N + (c + 1) * P)
+                    nc.tensor.matmul_mx(
+                        out=y[:, j, :],
+                        lhsT=w2_codes[m // 2][:, cols].bitcast(FP8X4),
+                        lhsT_scale=w2_scale[:, m * N + c * P : m * N + (c + 1) * P],
+                        rhs=h_codes[:].bitcast(FP8X4),
+                        rhs_scale=h_scale[:],
+                        start=True,
+                        stop=True,
+                    )
+                nc.scalar.copy(y_sb[:, b * halves : (b + 1) * halves, :], y[:])
             for c in range(N // P):
                 nc.vector.tensor_tensor(
                     results[c][:].indirect(entries(tok, m * SLOTS, SLOTS)),
@@ -168,13 +176,13 @@ def tile_moe_dyn_none_kernel(
         turn(0)
         gather_w2_words(0)
         quantise(0)
+        gather_w2_words(1)
         turn(1)
         first_product(2)
         quantise(1)
         second_product(0)
-        first_product(3)
-        gather_w2_words(1)
         turn(2)
+        first_product(3)
         quantise(2)
         second_product(1)
         turn(3)

@@ -1,7 +1,6 @@
 from contextlib import ExitStack
 
 import concourse.mybir as mybir
-from concourse.masks import make_identity
 
 K, T, E, B, H, N = 512, 512, 8, 4, 512, 256
 FLOPS = 2 * T * K * H + 2 * T * H * N
@@ -19,9 +18,7 @@ SLOTS = 128
 PER_COL = 16
 X_WINDOW = 768
 ROW_STEP = 8
-H_BANKS = (("a", "b"), ("c",), ("b",), ("f",))
-TURN_BANKS = ("d", "e", "a", "c")
-Y_BANKS = (("f", "g"), ("a",), ("c",), ("d",))
+Y_BANKS = (("y0", "y1"), ("y2",), ("y3",), ("y0",))
 
 
 def load_list(nc, pool, source, name):
@@ -58,13 +55,14 @@ def tile_moe_dyn_none_kernel(
     nc = tc.nc
     with ExitStack() as ctx:
         keep = ctx.enter_context(tc.tile_pool(name="keep", bufs=1))
+        handed_on = ctx.enter_context(tc.tile_pool(name="handed_on", bufs=1))
         psum = ctx.enter_context(tc.psum_pool(name="psum", bufs=1))
 
         x_plane = keep.tile([P, X_WINDOW], U8, align_bytes=64, tag="x_plane_then_w2_table")
         w1_plane = keep.tile([P, E * H], U8, align_bytes=64)
         w2_plane = keep.tile([P, E * N], U8, align_bytes=64, tag="w2_plane_then_gates")
         x_table = keep.tile([P, X_WINDOW], I32, align_bytes=64)
-        nc.vector.memset(x_plane[:].bitcast(I32), 0)
+        nc.vector.memset(x_plane[:, T:X_WINDOW].bitcast(I32), 0)
         nc.vector.memset(w1_plane[:].bitcast(I32), 0)
         nc.vector.memset(w2_plane[:].bitcast(I32), 0)
         nc.vector.memset(x_table[:, T:X_WINDOW], 0)
@@ -72,7 +70,9 @@ def tile_moe_dyn_none_kernel(
         tok = load_list(nc, keep, offs, "tok")
         col1 = load_list(nc, keep, offs2, "col1")
         col2 = load_list(nc, keep, offs3, "col2")
-        load_scale_rows(nc, x_plane, x_scales)
+        nc.sync.dma_start(
+            x_plane[:, 0:T].bitcast(I32), x_scales[0].bitcast(I32).unsqueeze(1).to_broadcast([16, ROW_STEP, T // 4])
+        )
         nc.sync.dma_start(x_table[:, 0:T], words_in_hbm(x_words))
         for r in range(4):
             nc.sync.dma_start(w1_plane[r:P:32, :].bitcast(I32), w1_scales[0, r:16:4, :].bitcast(I32))
@@ -80,57 +80,49 @@ def tile_moe_dyn_none_kernel(
         w1_table = keep.tile([P, E * H], I32, align_bytes=64)
         nc.sync.dma_start(w1_table[:], words_in_hbm(w1_words))
 
-        identity = keep.tile([P, P], F32)
-        make_identity(nc, identity[:])
 
         x_scale = gather_scales(nc, keep, x_plane, tok, "x")
         w2_table = keep.tile([P, E * N], I32, align_bytes=64, tag="x_plane_then_w2_table")
         nc.sync.dma_start(w2_table[:], words_in_hbm(w2_words))
         x_codes = keep.tile([P, T], U32, align_bytes=64)
         nc.vector.tensor_copy(x_codes[:], x_table[:].bitcast(U32).indirect(tok[:]))
-        w1_scale = keep.tile([P, B * H], U8, align_bytes=64)
-        nc.vector.tensor_copy(w1_scale[:], w1_plane[:].indirect(col1[:]))
+        w1_picked = keep.tile([P, B * H], U8, align_bytes=64)
+        nc.vector.tensor_copy(w1_picked[:], w1_plane[:].indirect(col1[:]))
         w2_scale = gather_scales(nc, keep, w2_plane, col2, "w2")
+        w1_scale = keep.tile([P, B * H], U8, align_bytes=64)
+        nc.vector.tensor_copy(
+            w1_scale[:].rearrange("p (m d q) -> p m d q", m=B, d=4), w1_picked[:].rearrange("p (m q d) -> p m d q", m=B, d=4)
+        )
         gates = keep.tile([P, T], F32, align_bytes=64, tag="w2_plane_then_gates")
         nc.sync.dma_start(gates[:], gate)
 
         w1_codes = []
         for m in range(B):
             codes = keep.tile([P, H], U32, align_bytes=64, name=f"w1_codes{m}", tag=f"w1_codes{m}")
-            nc.vector.tensor_copy(codes[:], w1_table[:].bitcast(U32).indirect(entries(col1, m * H, H)))
+            nc.vector.tensor_copy(codes[:].rearrange("p (d q) -> p q d", d=4), w1_table[:].bitcast(U32).indirect(entries(col1, m * H, H)))
             w1_codes.append(codes)
 
         results = [keep.tile([P, T], F32, align_bytes=64, name=f"result{c}") for c in range(N // P)]
-        rounded, grouped, quantised, w2_codes = {}, {}, {}, {}
+        grouped, quantised, w2_codes = {}, {}, {}
 
         def first_product(m):
             slots = slice(m * SLOTS, (m + 1) * SLOTS)
-            rounded[m] = keep.tile([P, H], BF16, align_bytes=64, name=f"rounded{m}", tag=f"rounded{m}")
-            parts = 2 if m == 0 else 1
-            width = H // parts
-            for part in range(parts):
-                bank = H_BANKS[m][part]
-                h_t = psum.tile([P, width], F32, name=f"h_t{m}{part}", tag=bank)
+            h = psum.tile([P, 4, SLOTS], F32, name=f"h{m}", tag=f"h{m}")
+            for d in range(4):
                 nc.tensor.matmul_mx(
-                    out=h_t[:],
-                    lhsT=x_codes[:, slots].bitcast(FP8X4),
-                    lhsT_scale=x_scale[:, slots],
-                    rhs=w1_codes[m][:, part * width : (part + 1) * width].bitcast(FP8X4),
-                    rhs_scale=w1_scale[:, m * H + part * width : m * H + (part + 1) * width],
+                    out=h[:, d, :],
+                    lhsT=w1_codes[m][:, d * P : (d + 1) * P].bitcast(FP8X4),
+                    lhsT_scale=w1_scale[:, m * H + d * P : m * H + (d + 1) * P],
+                    rhs=x_codes[:, slots].bitcast(FP8X4),
+                    rhs_scale=x_scale[:, slots],
                     start=True,
                     stop=True,
                 )
-                nc.scalar.copy(
-                    rounded[m][:].rearrange("s (u p e) -> s u p e", u=2, e=2)[:, :, part * width // 4 : (part + 1) * width // 4, :],
-                    h_t[:].rearrange("s (p u e) -> s u p e", u=2, e=2),
-                )
-
-        def turn(m):
-            turned = psum.tile([P, 2, SLOTS], F32, name=f"turned{m}", tag=TURN_BANKS[m])
-            for u in range(2):
-                nc.tensor.transpose(turned[:, u, :], rounded[m][:].bitcast(F32)[:, u * P : (u + 1) * P], identity[:])
-            grouped[m] = keep.tile([P, SLOTS * 4], BF16, align_bytes=64, name=f"grouped{m}", tag=(f"grouped{m}" if m < 2 else f"h_codes{m - 2}"))
-            nc.scalar.copy(grouped[m][:].bitcast(F32).rearrange("p (s u) -> p s u", u=2), turned[:].rearrange("p u s -> p s u"))
+            if m == 1:
+                grouped[m] = handed_on.tile([P, SLOTS * 4], BF16, align_bytes=64, name="grouped1", offset=8 * N - 4 * SLOTS)
+            else:
+                grouped[m] = keep.tile([P, SLOTS * 4], BF16, align_bytes=64, name=f"grouped{m}")
+            nc.scalar.copy(grouped[m][:].rearrange("p (s d) -> p s d", d=4), h[:].rearrange("p d s -> p s d"))
 
         def quantise(m):
             h_codes = keep.tile([P, SLOTS], U32, align_bytes=64, name=f"h_codes{m}", tag=f"h_codes{m}")
@@ -139,14 +131,11 @@ def tile_moe_dyn_none_kernel(
             quantised[m] = (h_codes, h_scale)
 
         def gather_w2_words(pair):
-            tag = "w2_codes0" if pair == 0 else "grouped0"
-            w2_codes[pair] = keep.tile([P, 2 * N], U32, align_bytes=64, name=f"w2_codes{pair}", tag=tag)
+            w2_codes[pair] = handed_on.tile([P, 2 * N], U32, align_bytes=64, name=f"w2_codes{pair}", offset=8 * N * pair)
             nc.vector.tensor_copy(w2_codes[pair][:], w2_table[:].bitcast(U32).indirect(entries(col2, pair * 2 * N, 2 * N)))
 
-        def second_product(m):
-            slots = slice(m * SLOTS, (m + 1) * SLOTS)
+        def second_product(m, y_sb, place):
             h_codes, h_scale = quantised[m]
-            y_sb = keep.tile([P, N // P, SLOTS], F32, name=f"y_sb{m}")
             halves = N // P // len(Y_BANKS[m])
             for b, bank in enumerate(Y_BANKS[m]):
                 y = psum.tile([P, halves, SLOTS], F32, name=f"y{m}{b}", tag=bank)
@@ -162,32 +151,32 @@ def tile_moe_dyn_none_kernel(
                         start=True,
                         stop=True,
                     )
-                nc.scalar.copy(y_sb[:, b * halves : (b + 1) * halves, :], y[:])
+                nc.scalar.copy(y_sb[:, b * halves : (b + 1) * halves, place * SLOTS : (place + 1) * SLOTS], y[:])
+
+        def finish(first, count):
+            y_sb = keep.tile([P, N // P, count * SLOTS], F32, name=f"y_sb{first}")
+            for place in range(count):
+                second_product(first + place, y_sb, place)
             for c in range(N // P):
                 nc.vector.tensor_tensor(
-                    results[c][:].indirect(entries(tok, m * SLOTS, SLOTS)),
+                    results[c][:].indirect(entries(tok, first * SLOTS, count * SLOTS)),
                     y_sb[:, c, :],
-                    gates[:, slots],
+                    gates[:, first * SLOTS : (first + count) * SLOTS],
                     mybir.AluOpType.mult,
                 )
 
         first_product(0)
-        first_product(1)
-        turn(0)
-        gather_w2_words(0)
         quantise(0)
-        gather_w2_words(1)
-        turn(1)
-        first_product(2)
+        first_product(1)
         quantise(1)
-        second_product(0)
-        turn(2)
-        first_product(3)
+        gather_w2_words(0)
+        gather_w2_words(1)
+        finish(0, 1)
+        first_product(2)
         quantise(2)
-        second_product(1)
-        turn(3)
+        finish(1, 1)
+        first_product(3)
         quantise(3)
-        second_product(2)
-        second_product(3)
+        finish(2, 2)
         for c in range(N // P):
             nc.sync.dma_start(out[c * P : (c + 1) * P, :], results[c][:])

@@ -68,12 +68,12 @@ def tile_moe_dyn_none_kernel(
         nc.vector.memset(x_table[:, T:X_WINDOW], 0)
 
         tok = load_list(nc, keep, offs, "tok")
-        col1 = load_list(nc, keep, offs2, "col1")
-        col2 = load_list(nc, keep, offs3, "col2")
         nc.sync.dma_start(
             x_plane[:, 0:T].bitcast(I32), x_scales[0].bitcast(I32).unsqueeze(1).to_broadcast([16, ROW_STEP, T // 4])
         )
+        col1 = load_list(nc, keep, offs2, "col1")
         nc.sync.dma_start(x_table[:, 0:T], words_in_hbm(x_words))
+        col2 = load_list(nc, keep, offs3, "col2")
         for r in range(4):
             nc.sync.dma_start(w1_plane[r:P:32, :].bitcast(I32), w1_scales[0, r:16:4, :].bitcast(I32))
         load_scale_rows(nc, w2_plane, w2_scales)
@@ -118,17 +118,22 @@ def tile_moe_dyn_none_kernel(
                     start=True,
                     stop=True,
                 )
-            if m == 1:
-                grouped[m] = handed_on.tile([P, SLOTS * 4], BF16, align_bytes=64, name="grouped1", offset=8 * N - 4 * SLOTS)
-            else:
-                grouped[m] = keep.tile([P, SLOTS * 4], BF16, align_bytes=64, name=f"grouped{m}")
-            nc.scalar.copy(grouped[m][:].rearrange("p (s d) -> p s d", d=4), h[:].rearrange("p d s -> p s d"))
+            nc.scalar.copy(grouped[m].rearrange("p (s d) -> p s d", d=4), h[:].rearrange("p d s -> p s d"))
 
-        def quantise(m):
-            h_codes = keep.tile([P, SLOTS], U32, align_bytes=64, name=f"h_codes{m}", tag=f"h_codes{m}")
-            h_scale = keep.tile([P, SLOTS], U8, align_bytes=64, name=f"h_scale{m}")
-            nc.vector.quantize_mx(out=h_codes[:].bitcast(FP8X4), scales=h_scale[:], in_=grouped[m][:])
-            quantised[m] = (h_codes, h_scale)
+        def first_layer(first, count):
+            if first == 1:
+                values = handed_on.tile([P, SLOTS * 4], BF16, align_bytes=64, name="grouped1", offset=8 * N - 4 * SLOTS)
+            else:
+                values = keep.tile([P, count * SLOTS * 4], BF16, align_bytes=64, name=f"grouped{first}")
+            for place in range(count):
+                grouped[first + place] = values[:, place * SLOTS * 4 : (place + 1) * SLOTS * 4]
+                first_product(first + place)
+            h_codes = keep.tile([P, count * SLOTS], U32, align_bytes=64, name=f"h_codes{first}")
+            h_scale = keep.tile([P, count * SLOTS], U8, align_bytes=64, name=f"h_scale{first}")
+            nc.vector.quantize_mx(out=h_codes[:].bitcast(FP8X4), scales=h_scale[:], in_=values[:])
+            for place in range(count):
+                part = slice(place * SLOTS, (place + 1) * SLOTS)
+                quantised[first + place] = (h_codes[:, part], h_scale[:, part])
 
         def gather_w2_words(pair):
             w2_codes[pair] = handed_on.tile([P, 2 * N], U32, align_bytes=64, name=f"w2_codes{pair}", offset=8 * N * pair)
@@ -146,8 +151,8 @@ def tile_moe_dyn_none_kernel(
                         out=y[:, j, :],
                         lhsT=w2_codes[m // 2][:, cols].bitcast(FP8X4),
                         lhsT_scale=w2_scale[:, m * N + c * P : m * N + (c + 1) * P],
-                        rhs=h_codes[:].bitcast(FP8X4),
-                        rhs_scale=h_scale[:],
+                        rhs=h_codes.bitcast(FP8X4),
+                        rhs_scale=h_scale,
                         start=True,
                         stop=True,
                     )
@@ -165,18 +170,13 @@ def tile_moe_dyn_none_kernel(
                     mybir.AluOpType.mult,
                 )
 
-        first_product(0)
-        quantise(0)
-        first_product(1)
-        quantise(1)
+        first_layer(0, 1)
+        first_layer(1, 1)
         gather_w2_words(0)
         gather_w2_words(1)
         finish(0, 1)
-        first_product(2)
-        quantise(2)
+        first_layer(2, 2)
         finish(1, 1)
-        first_product(3)
-        quantise(3)
         finish(2, 2)
         for c in range(N // P):
             nc.sync.dma_start(out[c * P : (c + 1) * P, :], results[c][:])

@@ -18,7 +18,10 @@ SLOTS = 128
 PER_COL = 16
 X_WINDOW = 768
 ROW_STEP = 8
-Y_BANKS = (("y0", "y1"), ("y2",), ("y3",), ("y0",))
+COPY = mybir.ActivationFunctionType.Copy
+MULT = mybir.AluOpType.mult
+LATER_W2_BYTES = 4 * 2 * N
+H_CODES_AT = {0: LATER_W2_BYTES - 256, 1: LATER_W2_BYTES + 1024, 2: LATER_W2_BYTES}
 
 
 def load_list(nc, pool, source, name):
@@ -55,12 +58,12 @@ def tile_moe_dyn_none_kernel(
     nc = tc.nc
     with ExitStack() as ctx:
         keep = ctx.enter_context(tc.tile_pool(name="keep", bufs=1))
-        handed_on = ctx.enter_context(tc.tile_pool(name="handed_on", bufs=1))
+        after_y0 = ctx.enter_context(tc.tile_pool(name="after_y0", bufs=1))
         psum = ctx.enter_context(tc.psum_pool(name="psum", bufs=1))
 
         x_plane = keep.tile([P, X_WINDOW], U8, align_bytes=64, tag="x_plane_then_w2_table")
         w1_plane = keep.tile([P, E * H], U8, align_bytes=64)
-        w2_plane = keep.tile([P, E * N], U8, align_bytes=64, tag="w2_plane_then_gates")
+        w2_plane = keep.tile([P, E * N], U8, align_bytes=64)
         x_table = keep.tile([P, X_WINDOW], I32, align_bytes=64)
         nc.vector.memset(x_plane[:, T:X_WINDOW].bitcast(I32), 0)
         nc.vector.memset(w1_plane[:].bitcast(I32), 0)
@@ -82,6 +85,8 @@ def tile_moe_dyn_none_kernel(
 
 
         x_scale = gather_scales(nc, keep, x_plane, tok, "x")
+        gates = keep.tile([P, T], F32, align_bytes=64)
+        nc.sync.dma_start(gates[:], gate)
         w2_table = keep.tile([P, E * N], I32, align_bytes=64, tag="x_plane_then_w2_table")
         nc.sync.dma_start(w2_table[:], words_in_hbm(w2_words))
         x_codes = keep.tile([P, T], U32, align_bytes=64)
@@ -93,8 +98,6 @@ def tile_moe_dyn_none_kernel(
         nc.vector.tensor_copy(
             w1_scale[:].rearrange("p (m d q) -> p m d q", m=B, d=4), w1_picked[:].rearrange("p (m q d) -> p m d q", m=B, d=4)
         )
-        gates = keep.tile([P, T], F32, align_bytes=64, tag="w2_plane_then_gates")
-        nc.sync.dma_start(gates[:], gate)
 
         w1_codes = []
         for m in range(B):
@@ -121,62 +124,87 @@ def tile_moe_dyn_none_kernel(
             nc.scalar.copy(grouped[m].rearrange("p (s d) -> p s d", d=4), h[:].rearrange("p d s -> p s d"))
 
         def first_layer(first, count):
-            if first == 1:
-                values = handed_on.tile([P, SLOTS * 4], BF16, align_bytes=64, name="grouped1", offset=8 * N - 4 * SLOTS)
-            else:
-                values = keep.tile([P, count * SLOTS * 4], BF16, align_bytes=64, name=f"grouped{first}")
+            values = keep.tile([P, count * SLOTS * 4], BF16, align_bytes=64, name=f"grouped{first}")
             for place in range(count):
                 grouped[first + place] = values[:, place * SLOTS * 4 : (place + 1) * SLOTS * 4]
                 first_product(first + place)
-            h_codes = keep.tile([P, count * SLOTS], U32, align_bytes=64, name=f"h_codes{first}")
+            return values
+
+        def quantise(first, count, values):
+            h_codes = after_y0.tile([P, count * SLOTS], U32, align_bytes=64, name=f"h_codes{first}", offset=H_CODES_AT[first])
             h_scale = keep.tile([P, count * SLOTS], U8, align_bytes=64, name=f"h_scale{first}")
             nc.vector.quantize_mx(out=h_codes[:].bitcast(FP8X4), scales=h_scale[:], in_=values[:])
             for place in range(count):
                 part = slice(place * SLOTS, (place + 1) * SLOTS)
                 quantised[first + place] = (h_codes[:, part], h_scale[:, part])
 
-        def gather_w2_words(pair):
-            w2_codes[pair] = handed_on.tile([P, 2 * N], U32, align_bytes=64, name=f"w2_codes{pair}", offset=8 * N * pair)
-            nc.vector.tensor_copy(w2_codes[pair][:], w2_table[:].bitcast(U32).indirect(entries(col2, pair * 2 * N, 2 * N)))
-
-        def second_product(m, y_sb, place):
-            h_codes, h_scale = quantised[m]
-            halves = N // P // len(Y_BANKS[m])
-            for b, bank in enumerate(Y_BANKS[m]):
-                y = psum.tile([P, halves, SLOTS], F32, name=f"y{m}{b}", tag=bank)
-                for j in range(halves):
-                    c = b * halves + j
-                    cols = slice((m % 2) * N + c * P, (m % 2) * N + (c + 1) * P)
-                    nc.tensor.matmul_mx(
-                        out=y[:, j, :],
-                        lhsT=w2_codes[m // 2][:, cols].bitcast(FP8X4),
-                        lhsT_scale=w2_scale[:, m * N + c * P : m * N + (c + 1) * P],
-                        rhs=h_codes.bitcast(FP8X4),
-                        rhs_scale=h_scale,
-                        start=True,
-                        stop=True,
-                    )
-                nc.scalar.copy(y_sb[:, b * halves : (b + 1) * halves, place * SLOTS : (place + 1) * SLOTS], y[:])
-
-        def finish(first, count):
-            y_sb = keep.tile([P, N // P, count * SLOTS], F32, name=f"y_sb{first}")
+        def gather_w2_words(first, count, codes):
+            nc.vector.tensor_copy(codes[:], w2_table[:].bitcast(U32).indirect(entries(col2, first * N, count * N)))
             for place in range(count):
-                second_product(first + place, y_sb, place)
-            for c in range(N // P):
-                nc.vector.tensor_tensor(
-                    results[c][:].indirect(entries(tok, first * SLOTS, count * SLOTS)),
-                    y_sb[:, c, :],
-                    gates[:, first * SLOTS : (first + count) * SLOTS],
-                    mybir.AluOpType.mult,
-                )
+                w2_codes[first + place] = codes[:, place * N : (place + 1) * N]
 
-        first_layer(0, 1)
-        first_layer(1, 1)
-        gather_w2_words(0)
-        gather_w2_words(1)
-        finish(0, 1)
-        first_layer(2, 2)
-        finish(1, 1)
-        finish(2, 2)
+        def second_product(m, c, y):
+            h_codes, h_scale = quantised[m]
+            nc.tensor.matmul_mx(
+                out=y,
+                lhsT=w2_codes[m][:, c * P : (c + 1) * P].bitcast(FP8X4),
+                lhsT_scale=w2_scale[:, m * N + c * P : m * N + (c + 1) * P],
+                rhs=h_codes.bitcast(FP8X4),
+                rhs_scale=h_scale,
+                start=True,
+                stop=True,
+            )
+
+        def half_products(first, count, c, bank):
+            y = psum.tile([P, count * SLOTS], F32, name=f"y{first}{c}", tag=bank)
+            for place in range(count):
+                second_product(first + place, c, y[:, place * SLOTS : (place + 1) * SLOTS])
+            return y
+
+        def places(c, first, count):
+            return results[c][:].indirect(entries(tok, first * SLOTS, count * SLOTS))
+
+        def gates_of(first, count):
+            return gates[:, first * SLOTS : (first + count) * SLOTS]
+
+        def scalar_scatter(c, first, count, values):
+            nc.scalar.activation(places(c, first, count), values, COPY)
+
+        def times_gate(first, count, y):
+            gated = keep.tile([P, count * SLOTS], F32, name=f"gated{first}")
+            nc.vector.tensor_tensor(gated[:], y[:], gates_of(first, count), MULT)
+            return gated
+
+        def copy_out(first, count, y):
+            plain = keep.tile([P, count * SLOTS], F32, name=f"plain{first}")
+            nc.scalar.copy(plain[:], y[:])
+            return plain
+
+        values0 = first_layer(0, 1)
+        values1 = first_layer(1, 1)
+        values23 = first_layer(2, 2)
+        quantise(0, 1, values0)
+        gather_w2_words(0, 1, keep.tile([P, N], U32, align_bytes=64, name="w2_codes0"))
+        gather_w2_words(1, 1, keep.tile([P, N], U32, align_bytes=64, name="w2_codes1"))
+        quantise(1, 1, values1)
+        y0 = psum.tile([P, N // P, SLOTS], F32, tag="y0")
+        for c in range(N // P):
+            second_product(0, c, y0[:, c, :])
+        plain1 = copy_out(1, 1, half_products(1, 1, 0, "y1"))
+        y11 = half_products(1, 1, 1, "y2")
+        gated0 = keep.tile([P, N // P, SLOTS], F32)
+        nc.vector.tensor_tensor(gated0[:], y0[:], gates_of(0, 1).unsqueeze(1).to_broadcast([P, N // P, SLOTS]), MULT)
+        gather_w2_words(2, 2, after_y0.tile([P, 2 * N], U32, align_bytes=64, name="w2_codes2", offset=0))
+        quantise(2, 2, values23)
+        for c in range(N // P):
+            scalar_scatter(c, 0, 1, gated0[:, c, :])
+        gated1 = times_gate(1, 1, y11)
+        plain2 = copy_out(2, 2, half_products(2, 2, 0, "y3"))
+        y21 = half_products(2, 2, 1, "h0")
+        nc.vector.tensor_tensor(places(0, 1, 1), plain1[:], gates_of(1, 1), MULT)
+        scalar_scatter(1, 1, 1, gated1[:])
+        gated2 = times_gate(2, 2, y21)
+        scalar_scatter(1, 2, 2, gated2[:])
+        nc.vector.tensor_tensor(places(0, 2, 2), plain2[:], gates_of(2, 2), MULT)
         for c in range(N // P):
             nc.sync.dma_start(out[c * P : (c + 1) * P, :], results[c][:])

@@ -63,7 +63,7 @@ def tile_moe_dyn_none_kernel(
 
         x_plane = keep.tile([P, X_WINDOW], U8, align_bytes=64, tag="x_plane_then_w2_table")
         w1_plane = keep.tile([P, E * H], U8, align_bytes=64)
-        w2_plane = keep.tile([P, E * N], U8, align_bytes=64)
+        w2_plane = keep.tile([P, E * N], U8, align_bytes=64, tag="w2_plane_then_gates")
         x_table = keep.tile([P, X_WINDOW], I32, align_bytes=64)
         nc.vector.memset(x_plane[:, T:X_WINDOW].bitcast(I32), 0)
         nc.vector.memset(w1_plane[:].bitcast(I32), 0)
@@ -85,8 +85,8 @@ def tile_moe_dyn_none_kernel(
 
 
         x_scale = gather_scales(nc, keep, x_plane, tok, "x")
-        gates = keep.tile([P, T], F32, align_bytes=64)
-        nc.sync.dma_start(gates[:], gate)
+        first_gates = keep.tile([P, SLOTS], F32, align_bytes=64)
+        nc.sync.dma_start(first_gates[:], gate[:, 0:SLOTS])
         w2_table = keep.tile([P, E * N], I32, align_bytes=64, tag="x_plane_then_w2_table")
         nc.sync.dma_start(w2_table[:], words_in_hbm(w2_words))
         x_codes = keep.tile([P, T], U32, align_bytes=64)
@@ -98,6 +98,8 @@ def tile_moe_dyn_none_kernel(
         nc.vector.tensor_copy(
             w1_scale[:].rearrange("p (m d q) -> p m d q", m=B, d=4), w1_picked[:].rearrange("p (m q d) -> p m d q", m=B, d=4)
         )
+        later_gates = keep.tile([P, T - SLOTS], F32, align_bytes=64, tag="w2_plane_then_gates")
+        nc.sync.dma_start(later_gates[:], gate[:, SLOTS:T])
 
         w1_codes = []
         for m in range(B):
@@ -165,7 +167,9 @@ def tile_moe_dyn_none_kernel(
             return results[c][:].indirect(entries(tok, first * SLOTS, count * SLOTS))
 
         def gates_of(first, count):
-            return gates[:, first * SLOTS : (first + count) * SLOTS]
+            if first == 0:
+                return first_gates[:]
+            return later_gates[:, (first - 1) * SLOTS : (first - 1 + count) * SLOTS]
 
         def scalar_scatter(c, first, count, values):
             nc.scalar.activation(places(c, first, count), values, COPY)
@@ -173,6 +177,17 @@ def tile_moe_dyn_none_kernel(
         def times_gate(first, count, y):
             gated = keep.tile([P, count * SLOTS], F32, name=f"gated{first}")
             nc.vector.tensor_tensor(gated[:], y[:], gates_of(first, count), MULT)
+            return gated
+
+        def both_halves(m):
+            y = psum.tile([P, N // P, SLOTS], F32, name=f"y{m}", tag=f"y{m}")
+            for c in range(N // P):
+                second_product(m, c, y[:, c, :])
+            return y
+
+        def both_halves_times_gate(m, y):
+            gated = keep.tile([P, N // P, SLOTS], F32, name=f"gated{m}")
+            nc.vector.tensor_tensor(gated[:], y[:], gates_of(m, 1).unsqueeze(1).to_broadcast([P, N // P, SLOTS]), MULT)
             return gated
 
         def copy_out(first, count, y):
@@ -187,22 +202,17 @@ def tile_moe_dyn_none_kernel(
         gather_w2_words(0, 1, keep.tile([P, N], U32, align_bytes=64, name="w2_codes0"))
         gather_w2_words(1, 1, keep.tile([P, N], U32, align_bytes=64, name="w2_codes1"))
         quantise(1, 1, values1)
-        y0 = psum.tile([P, N // P, SLOTS], F32, tag="y0")
-        for c in range(N // P):
-            second_product(0, c, y0[:, c, :])
-        plain1 = copy_out(1, 1, half_products(1, 1, 0, "y1"))
-        y11 = half_products(1, 1, 1, "y2")
-        gated0 = keep.tile([P, N // P, SLOTS], F32)
-        nc.vector.tensor_tensor(gated0[:], y0[:], gates_of(0, 1).unsqueeze(1).to_broadcast([P, N // P, SLOTS]), MULT)
+        gated0 = both_halves_times_gate(0, both_halves(0))
+        y1 = both_halves(1)
         gather_w2_words(2, 2, after_y0.tile([P, 2 * N], U32, align_bytes=64, name="w2_codes2", offset=0))
         quantise(2, 2, values23)
         for c in range(N // P):
             scalar_scatter(c, 0, 1, gated0[:, c, :])
-        gated1 = times_gate(1, 1, y11)
-        plain2 = copy_out(2, 2, half_products(2, 2, 0, "y3"))
-        y21 = half_products(2, 2, 1, "h0")
-        nc.vector.tensor_tensor(places(0, 1, 1), plain1[:], gates_of(1, 1), MULT)
-        scalar_scatter(1, 1, 1, gated1[:])
+        gated1 = both_halves_times_gate(1, y1)
+        plain2 = copy_out(2, 2, half_products(2, 2, 0, "y2"))
+        y21 = half_products(2, 2, 1, "y3")
+        nc.vector.tensor_copy(places(0, 1, 1), gated1[:, 0, :])
+        scalar_scatter(1, 1, 1, gated1[:, 1, :])
         gated2 = times_gate(2, 2, y21)
         scalar_scatter(1, 2, 2, gated2[:])
         nc.vector.tensor_tensor(places(0, 2, 2), plain2[:], gates_of(2, 2), MULT)

@@ -20,8 +20,6 @@ X_WINDOW = 768
 ROW_STEP = 8
 COPY = mybir.ActivationFunctionType.Copy
 MULT = mybir.AluOpType.mult
-LATER_W2_BYTES = 4 * 2 * N
-H_CODES_AT = {0: LATER_W2_BYTES - 256, 1: LATER_W2_BYTES + 1024, 2: LATER_W2_BYTES}
 
 
 def load_list(nc, pool, source, name):
@@ -58,7 +56,6 @@ def tile_moe_dyn_none_kernel(
     nc = tc.nc
     with ExitStack() as ctx:
         keep = ctx.enter_context(tc.tile_pool(name="keep", bufs=1))
-        after_y0 = ctx.enter_context(tc.tile_pool(name="after_y0", bufs=1))
         psum = ctx.enter_context(tc.psum_pool(name="psum", bufs=1))
 
         x_plane = keep.tile([P, X_WINDOW], U8, align_bytes=64, tag="x_plane_then_w2_table")
@@ -85,8 +82,8 @@ def tile_moe_dyn_none_kernel(
 
 
         x_scale = gather_scales(nc, keep, x_plane, tok, "x")
-        first_gates = keep.tile([P, SLOTS], F32, align_bytes=64)
-        nc.sync.dma_start(first_gates[:], gate[:, 0:SLOTS])
+        first_gates = keep.tile([P, 2 * SLOTS], F32, align_bytes=64)
+        nc.sync.dma_start(first_gates[:], gate[:, 0 : 2 * SLOTS])
         w2_table = keep.tile([P, E * N], I32, align_bytes=64, tag="x_plane_then_w2_table")
         nc.sync.dma_start(w2_table[:], words_in_hbm(w2_words))
         x_codes = keep.tile([P, T], U32, align_bytes=64)
@@ -98,8 +95,8 @@ def tile_moe_dyn_none_kernel(
         nc.vector.tensor_copy(
             w1_scale[:].rearrange("p (m d q) -> p m d q", m=B, d=4), w1_picked[:].rearrange("p (m q d) -> p m d q", m=B, d=4)
         )
-        later_gates = keep.tile([P, T - SLOTS], F32, align_bytes=64, tag="w2_plane_then_gates")
-        nc.sync.dma_start(later_gates[:], gate[:, SLOTS:T])
+        later_gates = keep.tile([P, 2 * SLOTS], F32, align_bytes=64, tag="w2_plane_then_gates")
+        nc.sync.dma_start(later_gates[:], gate[:, 2 * SLOTS : T])
 
         w1_codes = []
         for m in range(B):
@@ -132,18 +129,17 @@ def tile_moe_dyn_none_kernel(
                 first_product(first + place)
             return values
 
-        def quantise(first, count, values):
-            h_codes = after_y0.tile([P, count * SLOTS], U32, align_bytes=64, name=f"h_codes{first}", offset=H_CODES_AT[first])
-            h_scale = keep.tile([P, count * SLOTS], U8, align_bytes=64, name=f"h_scale{first}")
+        def quantise(first, count, values, codes_tag, scale_tag):
+            h_codes = keep.tile([P, count * SLOTS], U32, align_bytes=64, name=f"h_codes{first}", tag=codes_tag)
+            h_scale = keep.tile([P, count * SLOTS], U8, align_bytes=64, name=f"h_scale{first}", tag=scale_tag)
             nc.vector.quantize_mx(out=h_codes[:].bitcast(FP8X4), scales=h_scale[:], in_=values[:])
             for place in range(count):
                 part = slice(place * SLOTS, (place + 1) * SLOTS)
                 quantised[first + place] = (h_codes[:, part], h_scale[:, part])
 
-        def gather_w2_words(first, count, codes):
-            nc.vector.tensor_copy(codes[:], w2_table[:].bitcast(U32).indirect(entries(col2, first * N, count * N)))
-            for place in range(count):
-                w2_codes[first + place] = codes[:, place * N : (place + 1) * N]
+        def gather_w2_words(m, tag):
+            w2_codes[m] = keep.tile([P, N], U32, align_bytes=64, name=f"w2_codes{m}", tag=tag)
+            nc.vector.tensor_copy(w2_codes[m][:], w2_table[:].bitcast(U32).indirect(entries(col2, m * N, N)))
 
         def second_product(m, c, y):
             h_codes, h_scale = quantised[m]
@@ -157,37 +153,19 @@ def tile_moe_dyn_none_kernel(
                 stop=True,
             )
 
-        def half_products(first, count, c, bank):
-            y = psum.tile([P, count * SLOTS], F32, name=f"y{first}{c}", tag=bank)
-            for place in range(count):
-                second_product(first + place, c, y[:, place * SLOTS : (place + 1) * SLOTS])
-            return y
+        def bank(name, count, tag):
+            return psum.tile([P, count * SLOTS], F32, name=name, tag=tag)
 
         def places(c, first, count):
             return results[c][:].indirect(entries(tok, first * SLOTS, count * SLOTS))
 
         def gates_of(first, count):
-            if first == 0:
-                return first_gates[:]
-            return later_gates[:, (first - 1) * SLOTS : (first - 1 + count) * SLOTS]
-
-        def scalar_scatter(c, first, count, values):
-            nc.scalar.activation(places(c, first, count), values, COPY)
+            pair = (first_gates, later_gates)[first // 2]
+            return pair[:, first % 2 * SLOTS : (first % 2 + count) * SLOTS]
 
         def times_gate(first, count, y):
             gated = keep.tile([P, count * SLOTS], F32, name=f"gated{first}")
             nc.vector.tensor_tensor(gated[:], y[:], gates_of(first, count), MULT)
-            return gated
-
-        def both_halves(m):
-            y = psum.tile([P, N // P, SLOTS], F32, name=f"y{m}", tag=f"y{m}")
-            for c in range(N // P):
-                second_product(m, c, y[:, c, :])
-            return y
-
-        def both_halves_times_gate(m, y):
-            gated = keep.tile([P, N // P, SLOTS], F32, name=f"gated{m}")
-            nc.vector.tensor_tensor(gated[:], y[:], gates_of(m, 1).unsqueeze(1).to_broadcast([P, N // P, SLOTS]), MULT)
             return gated
 
         def copy_out(first, count, y):
@@ -195,26 +173,43 @@ def tile_moe_dyn_none_kernel(
             nc.scalar.copy(plain[:], y[:])
             return plain
 
+        def scalar_scatter(first, count, gated):
+            nc.scalar.activation(places(1, first, count), gated[:], COPY)
+
+        def vector_scatter(first, count, plain):
+            nc.vector.tensor_tensor(places(0, first, count), plain[:], gates_of(first, count), MULT)
+
         values0 = first_layer(0, 1)
         values1 = first_layer(1, 1)
         values23 = first_layer(2, 2)
-        quantise(0, 1, values0)
-        gather_w2_words(0, 1, keep.tile([P, N], U32, align_bytes=64, name="w2_codes0"))
-        gather_w2_words(1, 1, keep.tile([P, N], U32, align_bytes=64, name="w2_codes1"))
-        quantise(1, 1, values1)
-        gated0 = both_halves_times_gate(0, both_halves(0))
-        y1 = both_halves(1)
-        gather_w2_words(2, 2, after_y0.tile([P, 2 * N], U32, align_bytes=64, name="w2_codes2", offset=0))
-        quantise(2, 2, values23)
-        for c in range(N // P):
-            scalar_scatter(c, 0, 1, gated0[:, c, :])
-        gated1 = both_halves_times_gate(1, y1)
-        plain2 = copy_out(2, 2, half_products(2, 2, 0, "y2"))
-        y21 = half_products(2, 2, 1, "y3")
-        nc.vector.tensor_copy(places(0, 1, 1), gated1[:, 0, :])
-        scalar_scatter(1, 1, 1, gated1[:, 1, :])
-        gated2 = times_gate(2, 2, y21)
-        scalar_scatter(1, 2, 2, gated2[:])
-        nc.vector.tensor_tensor(places(0, 2, 2), plain2[:], gates_of(2, 2), MULT)
+        quantise(0, 1, values0, "h_codes0_then_w2_codes3", "h_scale0")
+        gather_w2_words(0, "w2_codes0")
+        gather_w2_words(1, "w2_codes1_then_h_codes2")
+        quantise(1, 1, values1, "h_codes1", "h_scale1")
+        gather_w2_words(2, "w2_codes2")
+        low01 = bank("low01", 2, "y0")
+        high0 = bank("high0", 1, "y1")
+        high1 = bank("high1", 1, "y2")
+        second_product(0, 1, high0[:])
+        second_product(0, 0, low01[:, 0:SLOTS])
+        second_product(1, 0, low01[:, SLOTS : 2 * SLOTS])
+        second_product(1, 1, high1[:])
+        gated0 = times_gate(0, 1, high0)
+        gather_w2_words(3, "h_codes0_then_w2_codes3")
+        gated1 = times_gate(1, 1, high1)
+        quantise(2, 2, values23, "w2_codes1_then_h_codes2", "h_scale2")
+        plain01 = copy_out(0, 2, low01)
+        scalar_scatter(0, 1, gated0)
+        scalar_scatter(1, 1, gated1)
+        low23 = bank("low23", 2, "y3")
+        high23 = bank("high23", 2, "h0")
+        for c, y in enumerate((low23, high23)):
+            for place in range(2):
+                second_product(2 + place, c, y[:, place * SLOTS : (place + 1) * SLOTS])
+        vector_scatter(0, 2, plain01)
+        plain23 = copy_out(2, 2, low23)
+        gated23 = times_gate(2, 2, high23)
+        scalar_scatter(2, 2, gated23)
+        vector_scatter(2, 2, plain23)
         for c in range(N // P):
             nc.sync.dma_start(out[c * P : (c + 1) * P, :], results[c][:])

@@ -183,33 +183,36 @@ def tile_moe_dyn_none_kernel(
         values1 = first_layer(1, 1)
         values23 = first_layer(2, 2)
         quantise(0, 1, values0, "h_codes0_then_w2_codes3", "h_scale0")
-        gather_w2_words(0, "w2_codes0")
-        gather_w2_words(1, "w2_codes1_then_h_codes2")
+        gather_w2_words(0, "w2_codes0_then_h_codes2")
+        gather_w2_words(1, "w2_codes1")
         quantise(1, 1, values1, "h_codes1", "h_scale1")
         gather_w2_words(2, "w2_codes2")
-        low01 = bank("low01", 2, "y0")
-        high0 = bank("high0", 1, "y1")
-        high1 = bank("high1", 1, "y2")
+        high0 = bank("high0", 1, "y0")
         second_product(0, 1, high0[:])
-        second_product(0, 0, low01[:, 0:SLOTS])
-        second_product(1, 0, low01[:, SLOTS : 2 * SLOTS])
+        low0 = bank("low0", 1, "y1")
+        second_product(0, 0, low0[:])
+        high1 = bank("high1", 1, "y2")
         second_product(1, 1, high1[:])
         gated0 = times_gate(0, 1, high0)
+        low1 = bank("low1", 1, "y0")
+        second_product(1, 0, low1[:])
         gather_w2_words(3, "h_codes0_then_w2_codes3")
+        quantise(2, 2, values23, "w2_codes0_then_h_codes2", "h_scale2")
         gated1 = times_gate(1, 1, high1)
-        quantise(2, 2, values23, "w2_codes1_then_h_codes2", "h_scale2")
-        plain01 = copy_out(0, 2, low01)
+        plain0 = copy_out(0, 1, low0)
         scalar_scatter(0, 1, gated0)
+        plain1 = copy_out(1, 1, low1)
         scalar_scatter(1, 1, gated1)
-        low23 = bank("low23", 2, "y3")
-        high23 = bank("high23", 2, "h0")
-        for c, y in enumerate((low23, high23)):
+        high23 = bank("high23", 2, "y3")
+        low23 = bank("low23", 2, "h0")
+        for c, y in ((1, high23), (0, low23)):
             for place in range(2):
                 second_product(2 + place, c, y[:, place * SLOTS : (place + 1) * SLOTS])
-        vector_scatter(0, 2, plain01)
-        plain23 = copy_out(2, 2, low23)
+        vector_scatter(0, 1, plain0)
         gated23 = times_gate(2, 2, high23)
+        vector_scatter(1, 1, plain1)
+        plain23 = copy_out(2, 2, low23)
         scalar_scatter(2, 2, gated23)
         vector_scatter(2, 2, plain23)
-        for c in range(N // P):
+        for c in (1, 0):
             nc.sync.dma_start(out[c * P : (c + 1) * P, :], results[c][:])

from contextlib import ExitStack

import concourse.mybir as mybir

K, T, E, B, H, N = 512, 512, 8, 4, 512, 256
FLOPS = 2 * T * K * H + 2 * T * H * N

F32 = mybir.dt.float32
BF16 = mybir.dt.bfloat16
I32 = mybir.dt.int32
U32 = mybir.dt.uint32
U16 = mybir.dt.uint16
U8 = mybir.dt.uint8
FP8X4 = mybir.dt.float8_e4m3fn_x4

P = 128
SLOTS = 128
PER_COL = 16
X_WINDOW = 768
ROW_STEP = 8
COPY = mybir.ActivationFunctionType.Copy
MULT = mybir.AluOpType.mult


def load_list(nc, pool, source, name):
    offsets = pool.tile(list(source.shape), U16, name=name)
    nc.sync.dma_start(offsets[:], source)
    return offsets


def entries(offsets, first, count):
    return offsets[:, first // PER_COL : (first + count) // PER_COL]


def words_in_hbm(words):
    return words[0].rearrange("p c d -> p (c d)").bitcast(I32)


def load_scale_rows(nc, plane, scales):
    nc.sync.dma_start(plane[0:P:ROW_STEP, 0 : scales.shape[2]].bitcast(I32), scales[0].bitcast(I32))


def gather_scales(nc, pool, plane, offsets, name):
    count = offsets.shape[1] * PER_COL
    rows = pool.tile([P, count], U8, align_bytes=64, name=f"{name}_rows")
    nc.vector.tensor_copy(rows[:], plane[:].indirect(offsets[:]))
    laid = pool.tile([P, count], U8, align_bytes=64, name=f"{name}_scale")
    for r in range(4):
        nc.sync.dma_start(laid[r:P:32, :].bitcast(I32), rows[ROW_STEP * r : P : 32, :].bitcast(I32))
    return laid


def tile_moe_dyn_none_kernel(
    tc, x_words, x_scales, w1_words, w1_scales, w2_words, w2_scales, gate, offs, offs2, offs3, out
):
    nc = tc.nc
    with ExitStack() as ctx:
        keep = ctx.enter_context(tc.tile_pool(name="keep", bufs=1))
        psum = ctx.enter_context(tc.psum_pool(name="psum", bufs=1))

        x_plane = keep.tile([P, X_WINDOW], U8, align_bytes=64, tag="x_plane_then_w2_table")
        w1_plane = keep.tile([P, E * H], U8, align_bytes=64)
        w2_plane = keep.tile([P, E * N], U8, align_bytes=64, tag="w2_plane_then_gates")
        x_table = keep.tile([P, X_WINDOW], I32, align_bytes=64)
        nc.vector.memset(x_plane[:, T:X_WINDOW].bitcast(I32), 0)
        nc.vector.memset(w1_plane[:].bitcast(I32), 0)
        nc.vector.memset(w2_plane[:].bitcast(I32), 0)
        nc.vector.memset(x_table[:, T:X_WINDOW], 0)

        tok = load_list(nc, keep, offs, "tok")
        nc.sync.dma_start(
            x_plane[:, 0:T].bitcast(I32), x_scales[0].bitcast(I32).unsqueeze(1).to_broadcast([16, ROW_STEP, T // 4])
        )
        col1 = load_list(nc, keep, offs2, "col1")
        nc.sync.dma_start(x_table[:, 0:T], words_in_hbm(x_words))
        col2 = load_list(nc, keep, offs3, "col2")
        for r in range(4):
            nc.sync.dma_start(w1_plane[r:P:32, :].bitcast(I32), w1_scales[0, r:16:4, :].bitcast(I32))
        load_scale_rows(nc, w2_plane, w2_scales)
        w1_table = keep.tile([P, E * H], I32, align_bytes=64)
        nc.sync.dma_start(w1_table[:], words_in_hbm(w1_words))


        x_scale = gather_scales(nc, keep, x_plane, tok, "x")
        first_gates = keep.tile([P, 2 * SLOTS], F32, align_bytes=64)
        nc.sync.dma_start(first_gates[:], gate[:, 0 : 2 * SLOTS])
        w2_table = keep.tile([P, E * N], I32, align_bytes=64, tag="x_plane_then_w2_table")
        nc.sync.dma_start(w2_table[:], words_in_hbm(w2_words))
        x_codes = keep.tile([P, T], U32, align_bytes=64)
        nc.vector.tensor_copy(x_codes[:], x_table[:].bitcast(U32).indirect(tok[:]))
        w1_picked = keep.tile([P, B * H], U8, align_bytes=64)
        nc.vector.tensor_copy(w1_picked[:], w1_plane[:].indirect(col1[:]))
        w2_scale = gather_scales(nc, keep, w2_plane, col2, "w2")
        w1_scale = keep.tile([P, B * H], U8, align_bytes=64)
        nc.vector.tensor_copy(
            w1_scale[:].rearrange("p (m d q) -> p m d q", m=B, d=4), w1_picked[:].rearrange("p (m q d) -> p m d q", m=B, d=4)
        )
        later_gates = keep.tile([P, 2 * SLOTS], F32, align_bytes=64, tag="w2_plane_then_gates")
        nc.sync.dma_start(later_gates[:], gate[:, 2 * SLOTS : T])

        w1_codes = []
        for m in range(B):
            codes = keep.tile([P, H], U32, align_bytes=64, name=f"w1_codes{m}", tag=f"w1_codes{m}")
            nc.vector.tensor_copy(codes[:].rearrange("p (d q) -> p q d", d=4), w1_table[:].bitcast(U32).indirect(entries(col1, m * H, H)))
            w1_codes.append(codes)

        results = [keep.tile([P, T], F32, align_bytes=64, name=f"result{c}") for c in range(N // P)]
        grouped, quantised, w2_codes = {}, {}, {}

        def first_product(m):
            slots = slice(m * SLOTS, (m + 1) * SLOTS)
            h = psum.tile([P, 4, SLOTS], F32, name=f"h{m}", tag=f"h{m}")
            for d in range(4):
                nc.tensor.matmul_mx(
                    out=h[:, d, :],
                    lhsT=w1_codes[m][:, d * P : (d + 1) * P].bitcast(FP8X4),
                    lhsT_scale=w1_scale[:, m * H + d * P : m * H + (d + 1) * P],
                    rhs=x_codes[:, slots].bitcast(FP8X4),
                    rhs_scale=x_scale[:, slots],
                    start=True,
                    stop=True,
                )
            nc.scalar.copy(grouped[m].rearrange("p (s d) -> p s d", d=4), h[:].rearrange("p d s -> p s d"))

        def first_layer(first, count):
            values = keep.tile([P, count * SLOTS * 4], BF16, align_bytes=64, name=f"grouped{first}")
            for place in range(count):
                grouped[first + place] = values[:, place * SLOTS * 4 : (place + 1) * SLOTS * 4]
                first_product(first + place)
            return values

        def quantise(first, count, values, codes_tag, scale_tag):
            h_codes = keep.tile([P, count * SLOTS], U32, align_bytes=64, name=f"h_codes{first}", tag=codes_tag)
            h_scale = keep.tile([P, count * SLOTS], U8, align_bytes=64, name=f"h_scale{first}", tag=scale_tag)
            nc.vector.quantize_mx(out=h_codes[:].bitcast(FP8X4), scales=h_scale[:], in_=values[:])
            for place in range(count):
                part = slice(place * SLOTS, (place + 1) * SLOTS)
                quantised[first + place] = (h_codes[:, part], h_scale[:, part])

        def gather_w2_words(m, tag):
            w2_codes[m] = keep.tile([P, N], U32, align_bytes=64, name=f"w2_codes{m}", tag=tag)
            nc.vector.tensor_copy(w2_codes[m][:], w2_table[:].bitcast(U32).indirect(entries(col2, m * N, N)))

        def second_product(m, c, y):
            h_codes, h_scale = quantised[m]
            nc.tensor.matmul_mx(
                out=y,
                lhsT=w2_codes[m][:, c * P : (c + 1) * P].bitcast(FP8X4),
                lhsT_scale=w2_scale[:, m * N + c * P : m * N + (c + 1) * P],
                rhs=h_codes.bitcast(FP8X4),
                rhs_scale=h_scale,
                start=True,
                stop=True,
            )

        def bank(name, count, tag):
            return psum.tile([P, count * SLOTS], F32, name=name, tag=tag)

        def places(c, first, count):
            return results[c][:].indirect(entries(tok, first * SLOTS, count * SLOTS))

        def gates_of(first, count):
            pair = (first_gates, later_gates)[first // 2]
            return pair[:, first % 2 * SLOTS : (first % 2 + count) * SLOTS]

        def times_gate(first, count, y):
            gated = keep.tile([P, count * SLOTS], F32, name=f"gated{first}")
            nc.vector.tensor_tensor(gated[:], y[:], gates_of(first, count), MULT)
            return gated

        def copy_out(first, count, y):
            plain = keep.tile([P, count * SLOTS], F32, name=f"plain{first}")
            nc.scalar.copy(plain[:], y[:])
            return plain

        def scalar_scatter(first, count, gated):
            nc.scalar.activation(places(1, first, count), gated[:], COPY)

        def vector_scatter(first, count, plain):
            nc.vector.tensor_tensor(places(0, first, count), plain[:], gates_of(first, count), MULT)

        values0 = first_layer(0, 1)
        values1 = first_layer(1, 1)
        values23 = first_layer(2, 2)
        quantise(0, 1, values0, "h_codes0_then_w2_codes3", "h_scale0")
        gather_w2_words(0, "w2_codes0_then_h_codes2")
        gather_w2_words(1, "w2_codes1")
        quantise(1, 1, values1, "h_codes1", "h_scale1")
        gather_w2_words(2, "w2_codes2")
        high0 = bank("high0", 1, "y0")
        second_product(0, 1, high0[:])
        low0 = bank("low0", 1, "y1")
        second_product(0, 0, low0[:])
        high1 = bank("high1", 1, "y2")
        second_product(1, 1, high1[:])
        gated0 = times_gate(0, 1, high0)
        low1 = bank("low1", 1, "y0")
        second_product(1, 0, low1[:])
        gather_w2_words(3, "h_codes0_then_w2_codes3")
        quantise(2, 2, values23, "w2_codes0_then_h_codes2", "h_scale2")
        gated1 = times_gate(1, 1, high1)
        plain0 = copy_out(0, 1, low0)
        scalar_scatter(0, 1, gated0)
        plain1 = copy_out(1, 1, low1)
        scalar_scatter(1, 1, gated1)
        high23 = bank("high23", 2, "y3")
        low23 = bank("low23", 2, "h0")
        for c, y in ((1, high23), (0, low23)):
            for place in range(2):
                second_product(2 + place, c, y[:, place * SLOTS : (place + 1) * SLOTS])
        vector_scatter(0, 1, plain0)
        gated23 = times_gate(2, 2, high23)
        vector_scatter(1, 1, plain1)
        plain23 = copy_out(2, 2, low23)
        scalar_scatter(2, 2, gated23)
        vector_scatter(2, 2, plain23)
        for c in (1, 0):
            nc.sync.dma_start(out[c * P : (c + 1) * P, :], results[c][:])
